import numpy as np, ml_dtypes
CORES = [51,54,179,182]
N = 4
BF = ml_dtypes.bfloat16
V, Q, RO = 768, 4, 2
W = N * V
def parts(rng):
    big = rng.permutation(np.array([1.0, 1.0, 0.8, 0.8, 0.65, 0.65, 0.5, 0.5])).reshape(1, 8, 1, 1)
    am = (256 * big * rng.random((N, 8, 1, V)) * rng.random((N, 8, 16, V))).astype(np.int64)
    o = rng.permutation(8); w = np.array([12, 12, 40, 40, 80, 80, 128, 128])[o].reshape(1, 8, 1, 1); mid = np.array([10, 10, 32, 32, 57, 57, 64, 64])[o].reshape(1, 8, 1, 1)
    ph = rng.integers(-w, w + 1, (N, 8, 16, V)) & 255
    th = np.clip((mid * (0.9 + 0.2 * rng.random((N, 8, 1, 1)))).astype(np.int64) + rng.integers(-3, 4, (N, 8, 16, 1)), 0, 128)
    return am, ph, rng.integers(0, W, (N, 8, 16, V)), th
def pack(am, ph, tr, th):
    return {"amp": np.ascontiguousarray(am.reshape(N, 128, V)).astype(np.int32), "phi": np.ascontiguousarray(ph.reshape(N, 128, V)).astype(np.int32),
            "tri": np.ascontiguousarray(tr.reshape(N, 128, V)).astype(np.int32), "th": np.ascontiguousarray(th.reshape(N, 128, 1)).astype(np.int32)}
def setup_inputs(rng):
    return pack(*parts(rng))
def setup_inputs_ties(rng):
    am, ph, tr, th = parts(rng)
    am[:, :4] = rng.permutation(np.array([0, 1, 8, 255])).reshape(1, 4, 1, 1); am[:, 4:] = 64 * rng.integers(0, 2, (N, 4, 1, V))
    p = rng.permutation(np.array([0, 1, 127, 128, 129, 255, 64, 37])); size = np.abs(((p + 128) & 255) - 128)
    ph[:] = p.reshape(1, 8, 1, 1); th[:] = size.reshape(1, 8, 1, 1); th[1::2, :, int(rng.integers(0, 16)), 0] = np.maximum(size - 1, 0)
    return pack(am, ph, tr, th)
def setup_inputs_harsh(rng):
    am, ph, tr, th = parts(rng); g = rng.permutation(8); i = int(rng.integers(0, 16))
    am[:, g[1]] = 255; am[:, g[2]] = rng.integers(0, 3, (N, 16, V)); am[:, g[2], i] = rng.integers(0, 256, (N, V))
    am[int(rng.integers(0, N))] = 0; am[:, g[0]] = 0
    th[:, g[1:]] = rng.permutation(np.array([0, 0, 0, 128, 128, 5, 30])).reshape(1, 7, 1, 1)
    return pack(am, ph, tr, th)
def setup_inputs_ends(rng):
    am, ph, tr, th = parts(rng); own = np.arange(N)[:, None, None] * V + np.arange(V)[None, None, :]
    tr[:, 0] = rng.choice(np.array([0, V - 1, V, W - V, W - 1]), (N, 16, V))
    tr[:, 1, 0::2] = own
    tr[:, 2] = ((np.arange(N) + 1) % N)[:, None, None] * V + rng.integers(0, V, (N, 16, V))
    tr[:, 3, 1::2] = tr[:, 3, 0::2]
    tr[:, 4, 2::2] = tr[:, 4, 0:1]; tr[:, 4, 3::2] = tr[:, 4, 1:2]
    tr[:, 5] = own - own % Q + rng.integers(0, Q, (N, 16, V))
    return pack(am, ph, tr, th)
def setup_inputs_bright(rng):
    am, ph, tr, th = parts(rng); own = np.arange(W).reshape(N, 1, V); g = rng.permutation(8)
    sign = rng.permutation(np.array([1, -1] * 8)).reshape(1, 1, 16, 1)
    tr[:, g[:5]] = Q * rng.integers(0, W // Q, (N, 5, 16, V)) + Q - 1
    am[:, g[:5]] = rng.integers(0, 41, (1, 5, 16, 1))
    ph[:, g[:3]] = (sign * rng.integers(105, 116, (N, 3, 16, V))) & 255
    ph[:, g[3:5]] = (sign * rng.integers(62, 67, (N, 2, 16, V))) & 255
    ph[:, g[5:]] = rng.integers(-8, 9, (N, 3, 16, V)) & 255
    th[:] = 128; th[:, g[2]] = 0; th[:, g[3], :8] = 0; th[:, g[4], 8:] = 0
    for c in g[5:]:
        lose = (np.arange(Q) == rng.integers(0, Q - 1, (W // Q, 1))).reshape(W)
        live = np.flatnonzero(~lose); lose = lose.reshape(N, 1, V)
        am[:, c] = np.where(lose, rng.integers(236, 241, (N, 16, V)), rng.integers(246, 256, (N, 16, V)))
        x = live[rng.integers(0, live.size, (N, 16, V))]
        x[:, 0::2] = np.where(lose, own, x[:, 0::2])
        tr[:, c] = x
    return pack(am, ph, tr, th)
def setup_inputs_spread(rng):
    am, ph, tr, th = parts(rng)
    am = np.minimum((np.exp2(8 * rng.random((N, 8, 1, V))) * rng.random((N, 8, 16, V))).astype(np.int64), 255)
    ph = np.floor(np.exp2(7 * rng.random((N, 8, 1, V))) * (2 * rng.random((N, 8, 16, V)) - 1)).astype(np.int64) & 255
    tr = np.minimum((W * rng.random((N, 8, 16, V)) ** 3).astype(np.int64), W - 1)
    th = np.minimum(np.exp2(7 * rng.random((N, 8, 16, 1))).astype(np.int64), 128)
    return pack(am, ph, tr, th)
def check_inputs(d):
    bad = []
    for k, lo, hi in (("amp", 0, 255), ("phi", 0, 255), ("tri", 0, W - 1), ("th", 0, 128)):
        if np.min(d[k]) < lo or np.max(d[k]) > hi: bad.append("range of " + k)
    return bad
def flat(x):
    return np.ascontiguousarray(x.astype(np.int64).reshape(N, 8, 16, V).transpose(1, 2, 0, 3)).reshape(8, 16, W)
def reference(amp, phi, tri, th):
    a0, trial, tr, lim = flat(amp), flat(phi), flat(tri), flat(np.repeat(th, V, axis=2))
    rej = np.zeros((8, W), bool)
    for rnd in range(RO):
        a = np.where(rej[:, None, :], 0, a0); lev = np.full((8, W), Q - 1)
        for t in range(Q - 1):
            s = np.zeros((8, 16, W), np.int64)
            for g in range(8):
                for m in range(8): s[g] += np.minimum(a[g][:, tr[g, 2 * m]], a[g][:, tr[g, 2 * m + 1]])
            tot = np.where(rej, -1, np.add.reduce(s, axis=1))
            tot = np.where(lev == Q - 1, tot, 2 ** 24)
            first = np.argmin(tot.reshape(8, W // Q, Q), axis=2)
            gone = (np.arange(Q) == first[:, :, None]).reshape(8, W)
            lev = np.where(gone, t, lev)
            both = np.add.reduce(s, axis=0)
            a = np.where(gone[:, None, :], 0, np.minimum(np.minimum(a, s >> 3), both >> 5))
        p = np.array(trial); phased = lev == Q - 1; fail = np.zeros((8, W), bool)
        for t in range(Q - 2, -1, -1):
            at = np.stack([np.flatnonzero(lev[g] == t) for g in range(8)])
            total = np.zeros((8, 16, W // Q), np.int64); x = np.zeros((8, 16, W // Q), np.int64)
            for g in range(8):
                h = at[g]; c = trial[g][:, h]
                for m in range(8):
                    k, l = tr[g, 2 * m][h], tr[g, 2 * m + 1][h]
                    v = (phased[g][k] & phased[g][l]).astype(np.int64)
                    dl = ((p[g][:, k] + p[g][:, l] - c + 128) & 255) - 128
                    total[g] += v * dl; x[g] += v * (np.abs(dl) - lim[g][:, h])
            y = np.add.reduce(total, axis=0)
            u = (total + (y >> 3)) >> 3
            for g in range(8):
                h = at[g]; c = trial[g][:, h]; no = np.add.reduce(x[g], axis=0) > 0
                p[g][:, h] = np.where(no, c, (c + u[g]) & 255)
                phased[g][h] = ~no; fail[g][h] = no
        rej = rej | fail
    yphi = np.ascontiguousarray(p.reshape(8, 16, N, V).transpose(2, 0, 1, 3)).reshape(N, 128, V)
    ylev = np.ascontiguousarray(lev.reshape(8, N, V).transpose(1, 0, 2))
    return {"yphi": yphi.astype(np.float32), "ylev": ylev.astype(np.float32)}

@@ -1,0 +1,668 @@
+from concourse.bass import DstId, RemoteDMATransfer
+from concourse.mybir import AluOpType, ActivationFunctionType
+
+NV, NW = 768, 3072
+GR = [(0, 8), (8, 12)]
+NS = 2
+TWO = (1, 2, 7, 8)
+OFF = 1088.0
+MARK = float(2 ** 42)
+BF, F16, F32, I32, U16 = "bfloat16", "float16", "float32", "int32", "uint16"
+
+SCRATCH = {}
+PART = {}
+
+
+def _sb(dt, cols, names):
+    for n in names.split():
+        SCRATCH[n] = ("sbuf", [128, cols], dt)
+
+
+def _pack(base, dt, names):
+    for i, n in enumerate(names.split()):
+        PART[n] = (base, 16 * i)
+    _sb(dt, 16 * len(names.split()), base)
+
+
+_sb(I32, NV, "amp32 phi32 tri32")
+_sb(I32, 1, "th32")
+_sb(F32, 1, "thf")
+_sb(BF, NW, " ".join("tab%d" % i for i in range(12)))
+_sb(BF, 6144, "ga mn")
+_sb(BF, 1536, "zb db ab tb")
+_sb(U16, 384, "offa offb")
+_sb(U16, 192, "lx ly e0 e1 e2")
+_sb(F16, NV, "r16 a16 x1 x2 sf sr ur r1")
+_sb(F32, NV, "scn pout lev")
+_sb(BF, NV, "phib dp0 dp1")
+_sb(F16, 192, "glo ghi rr")
+_sb(BF, 192, "bd c0 c1 c2 ag0 ag1 ag2 zz pb mk nk dd")
+_sb(F32, 192, "cf0 cf1 cf2 tt r16s sc2")
+_sb(F32, 512, "r64")
+_sb(BF, 512, "ke kc")
+_sb(BF, 128, "oneb moneb eight ib nib i8 gt gp gn b1 lu s64 ks kl zero mark big")
+_sb(F16, 128, "de do se so b512 bh g512 s32 ih nih")
+_sb(F32, 128, "l0 l1 l2 bhi bhs")
+_pack("smi", I32, "mi si0 si1 si2 j0 j1 b4")
+_pack("smu", U16, "su0 su1 su2 lou hiu")
+_pack("smf", F32, "w0 w1 w2 w3 lo hi lop hip k0 k1 k2 f0 f1 fm fx y2")
+for _i in range(8):
+    SCRATCH["ps%d" % _i] = ("psum", [128, 512], F32)
+
+SEMAPHORES = (["sv", "sa", "sp", "sg", "sent", "d_amp", "d_tri", "d_phi", "d_th", "d_y0", "d_y1", "d_lev"]
+              + ["arr%d" % i for i in range(12)])
+QSEM = {"v": "sv", "a": "sa", "p": "sp", "g": "sg"}
+OP = AluOpType
+AF = ActivationFunctionType
+
+
+def A(name, c0=0, c1=None, step=1, p0=0, p1=128):
+    if name in PART:
+        base, o = PART[name]
+        return (base, o + c0, o + (12 if c1 is None else c1), step, p0, p1)
+    if c1 is None:
+        c1 = SCRATCH[name][1][1]
+    return (name, c0, c1, step, p0, p1)
+
+
+def IND(win, off):
+    return ("*", win, off)
+
+
+def rank_program(g, core, T, topo):
+    rank = T.rank_of(core)
+    if rank is None:
+        return
+    ops = []
+
+    def ap(d):
+        if not isinstance(d, tuple):
+            return d
+        if d[0] == "*":
+            return ap(d[1]).indirect(ap(d[2]))
+        n, c0, c1, st, p0, p1 = d
+        t = T[n]
+        if p0 == 0 and p1 == 128:
+            return t[:, c0:c1] if st == 1 else t[:, c0:c1:st]
+        return t[p0:p1, c0:c1] if st == 1 else t[p0:p1, c0:c1:st]
+
+    def rec(q, fn, outs, ins, ext=None, sem=None):
+        rd, wr = [], []
+        for d in outs:
+            if d[0] == "*":
+                wr.append(d[1]); rd.append(d[2])
+            else:
+                wr.append(d)
+        for d in ins:
+            if isinstance(d, tuple):
+                if d[0] == "*":
+                    rd.append(d[1]); rd.append(d[2])
+                else:
+                    rd.append(d)
+        ops.append({"q": q, "fn": fn, "rd": rd, "wr": wr, "ext": ext, "sem": sem})
+
+    def cp(o, i, ext=None):
+        rec("v", lambda: g.vector.tensor_copy(ap(o), ap(i)), [o], [i], ext)
+
+    def tt(o, a, b, op, ext=None):
+        rec("v", lambda: g.vector.tensor_tensor(ap(o), ap(a), ap(b), op), [o], [a, b], ext)
+
+    def ts(o, a, s1, op0, s2=None, op1=None):
+        if op1 is None:
+            rec("v", lambda: g.vector.tensor_scalar(ap(o), ap(a), ap(s1), None, op0), [o], [a, s1])
+        else:
+            rec("v", lambda: g.vector.tensor_scalar(ap(o), ap(a), ap(s1), ap(s2), op0, op1), [o], [a, s1, s2])
+
+    def ms(o, val):
+        rec("v", lambda: g.vector.memset(ap(o), val), [o], [])
+
+    def scan(o, d0, d1, op1):
+        rec("v", lambda: g.vector.tensor_tensor_scan(ap(o), ap(d0), ap(d1), 0.0, OP.add, op1), [o], [d0, d1])
+
+    def act(o, i, func=AF.Copy, bias=0.0, scale=1.0, ext=None):
+        rec("a", lambda: g.scalar.activation(ap(o), ap(i), func, bias=bias, scale=scale), [o], [i], ext)
+
+    def mm(o, l, r, start, stop):
+        rec("p", lambda: g.tensor.matmul(ap(o), ap(l), ap(r), start, stop), [o], [l, r])
+
+    def sel(o, i, pat, cmp, fill, base, cm):
+        rec("g", lambda: g.affine_select(ap(o), ap(i), pat, cmp, fill, base, cm), [o], [i])
+
+    def load(o, src, sem):
+        rec("s", lambda: g.sync.dma_start(ap(o), src), [o], [], sem=sem)
+
+    def store(dst, i, sem):
+        rec("s", lambda: g.sync.dma_start(dst, ap(i)), [], [i], sem=sem)
+
+    peers = [c for c in T.cores if c != core]
+    near = [c for c in peers if c in topo.cores_of(core)]
+    far = [c for c in peers if c not in near]
+    off_eng = topo.engines(core, far[0])
+    on_eng = [e for e in topo.engines(core, near[0]) if e not in off_eng]
+    share = len(off_eng) // len(far)
+    masks = {near[0]: sum(1 << e for e in on_eng)}
+    for i, c in enumerate(far):
+        masks[c] = sum(1 << e for e in off_eng[i * share:(i + 1) * share])
+    per_send = len(on_eng) + share * len(far)
+    nsent = [0]
+
+    def own(k, c0=0, c1=12):
+        return A("tab%d" % k, rank * NV + 64 * c0, rank * NV + 64 * c1)
+
+    def send(k, c0=0, c1=12):
+        d = own(k, c0, c1)
+
+        def fn():
+            trs = []
+            for c in far + near:
+                rid, pid = topo.addr(c, core)
+                trs.append(RemoteDMATransfer(dst_ids=[DstId(rid=rid, pnc=pid)], dma_engine_mask=masks[c],
+                                             remote_sem=T.sem["arr%d" % k], src=ap(d), dst=ap(d)))
+            g.remote_dma_fused(trs, local_sem=T.sem.sent)
+        nsent[0] += per_send
+        rec("g", fn, [], [d], sem="none")
+
+    def send_group(k, gi):
+        if k in TWO:
+            send(k, *GR[gi])
+        elif gi == 1:
+            send(k)
+
+    def arrived(k):
+        return ("arr%d" % k, per_send * (len(GR) if k in TWO else 1))
+
+    def gc_(name, gi, per):
+        return A(name, per * GR[gi][0], per * GR[gi][1])
+
+    def gn(gi, per):
+        return per * (GR[gi][1] - GR[gi][0])
+
+    def scatter_const(win, t, src):
+        for gi in range(2):
+            cp(IND(win(gi), gc_("su%d" % t, gi, 1)), A(src, 0, gn(gi, 16)))
+
+    load(A("amp32"), T.amp[:], "d_amp")
+    load(A("tri32"), T.tri[:], "d_tri")
+    load(A("phi32"), T.phi[:], "d_phi")
+    load(A("th32"), T.th[:], "d_th")
+    ms(A("oneb"), 1.0)
+    ms(A("eight"), 0.125)
+    picks = (("de", 200, 0), ("do", -200, 199), ("se", 200, -1), ("so", -200, 200))
+    for i, (n, st, base) in enumerate(picks):
+        sel(A("mn", 128 * i, 128 * i + 128), A("oneb"), [[-2, 64], [st, 2]], OP.is_equal, 0.0, base, 1)
+    sel(A("i8"), A("eight"), [[-1, 128]], OP.is_equal, 0.0, 0, 1)
+    sel(A("b1", p1=16), A("oneb", p1=16), [[0, 8], [-1, 16]], OP.is_equal, 0.0, 0, 1)
+    ms(A("moneb"), -1.0)
+    rows = (("ks", OFF, -31.0 / 64), ("kl", 50688.0, -63.0 / 128))
+    for n, a, b in rows:
+        ms(A(n, p1=64), 0.0)
+    ms(A("ke", p1=64), 0.0)
+    ms(A("zero"), 0.0)
+    ms(A("bd", p1=32), 0.0)
+    ms(A("r64"), 0.0)
+    ms(A("r16s"), 0.0)
+    for n, a, b in rows:
+        ms(A(n, p1=1), a)
+        ms(A(n, p0=32, p1=33), b)
+    ms(A("ke", p1=1), 49152.0)
+    ms(A("r64", 0, 512, 64), float(2 ** 26))
+    ms(A("r16s", 0, 192, 16), -float(2 ** 28))
+    ms(A("kc", 0, 128, p1=1), -OFF)
+    for i in range(1, 4):
+        ms(A("kc", 128 * i, 128 * i + 128, p1=1), 128.0 * i)
+    ms(A("mark"), MARK)
+    ms(A("big"), float(2 ** 25))
+    for i, (n, st, base) in enumerate(picks):
+        cp(A(n), A("mn", 128 * i, 128 * i + 128))
+    cp(own(0), A("amp32"))
+    send(0)
+    ts(A("r16"), A("tri32"), -1536.0, OP.add)
+    sel(A("ib"), A("oneb"), [[-1, 128]], OP.is_equal, 0.0, 0, 1)
+    sel(A("nib"), A("moneb"), [[-1, 128]], OP.is_equal, 0.0, 0, 1)
+    sel(A("gt"), A("oneb"), [[-16, 8], [0, 16]], OP.is_ge, 0.0, 0, 1)
+    sel(A("gt"), A("gt"), [[16, 8], [0, 16]], OP.is_ge, 0.0, 15, -1)
+    rec("g", lambda: g.iota(ap(A("bhi", p1=16)), [[1, 128]], 0, 0, allow_small_or_imprecise_dtypes=True),
+        [A("bhi", p1=16)], [])
+    sel(A("bhs", p1=16), A("bhi", p1=16), [[0, 2], [-1, 16], [0, 4]], OP.is_equal, 60000.0 * 512, 0, 1)
+    sel(A("bd", p1=16), A("bd", p1=16), [[0, 12], [-1, 16]], OP.is_equal, -float(2 ** 27), 0, 1)
+    for bank, l0, l1 in (("ps6", "de", "do"), ("ps7", "se", "so")):
+        for k in range(6):
+            mm(A(bank, 64 * k, 64 * k + 64), A(l0), A("r16", 128 * k, 128 * k + 64), True, False)
+            mm(A(bank, 64 * k, 64 * k + 64), A(l1), A("r16", 128 * k + 64, 128 * k + 128), False, True)
+    mm(A("ps5", 0, 128), A("b1", p1=16), A("b1", p1=16), True, True)
+
+    def prep_a16(k):
+        act(A("a16", 128 * NS, NV), own(k, 2 * NS, 12), AF.Identity, bias=OFF)
+
+    prep_a16(0)
+    ts(A("offa"), A("ps6", 0, 384), 1536.0, OP.add)
+    ts(A("offb"), A("ps7", 0, 384), 1536.0, OP.add)
+    ts(A("s32"), A("ps5", 0, 128), 1.0 / 32, OP.mult)
+    ts(A("s64"), A("ps5", 0, 128), 1.0 / 64, OP.mult)
+    ts(A("b512", p1=16), A("b1", p1=16), 512.0, OP.mult)
+    cp(A("phib"), A("phi32"))
+    cp(A("thf"), A("th32"))
+    ms(A("dp0"), 0.0)
+    tt(A("lu"), A("s64"), A("i8"), OP.add)
+    cp(A("ih"), A("ib"))
+    cp(A("nih"), A("nib"))
+    ts(A("g512"), A("gt"), 512.0, OP.mult)
+    ts(A("gp"), A("gt"), 1024.0, OP.mult)
+    ts(A("gn"), A("gt"), -1024.0, OP.mult)
+    ts(A("bh", p1=16), A("bhs", p1=16), 1.0 / 512, OP.mult)
+
+    def K33(n, w):
+        return A(n, 0, w, p1=33)
+    ONE33 = A("oneb", p1=33)
+    DOWN = OFF - 31.0 / 64
+
+    def round01(pas, t, kin, kout):
+        tab = A("tab%d" % kin)
+        ext = arrived(kin)
+
+        def sg(x0, x1):
+            act(A("ga", 16 * x0, 16 * x1), IND(tab, A("offa", x0, x1)), ext=ext)
+
+        def vg(x0, x1):
+            tt(A("mn", 16 * x0, 16 * x1), IND(tab, A("offb", x0, x1)), A("ga", 16 * x0, 16 * x1), OP.min, ext=ext)
+
+        def pc(n, k, k1=None):
+            return A(n, 128 * k, 128 * (k + 1 if k1 is None else k1))
+
+        def sbank(k):
+            return A("ps%d" % (k % 3), 0, 128)
+
+        def bank(first, k):
+            gi = 0 if 2 * k < GR[0][1] else 1
+            o = 128 * k - 64 * GR[gi][0]
+            return A("ps%d" % (first + gi), o, o + 128)
+
+        def ssum(k):
+            b = "ps%d" % (k % 3)
+            if k >= NS:
+                mm(sbank(k), ONE33, K33("ks", 128), True, False)
+            for e in range(2):
+                for m in range(8):
+                    mm(A(b, 64 * e, 64 * e + 64), A("i8"), A("mn", 1024 * k + 2 * m + e, 1024 * k + 1024, 16),
+                       k < NS and m == 0, m == 7 and (k < NS or e == 1))
+
+        def copy(k):
+            w, u = bank(5, k), bank(3, k)
+            mm(w, A("b512", p1=16), A("bh", p1=16), True, False)
+            if w[1]:
+                mm(w, A("oneb", p1=1), A("kc", w[1], w[2], p1=1), False, False)
+            if t == 1:
+                mm(w, A("ib"), pc("dp%d" % pas, k), False, False)
+            if k >= NS:
+                mm(u, ONE33, K33("ks", 128), True, False)
+            if k == 5:
+                ts(pc("sf", k), sbank(k), 8.0, OP.mult, -8 * DOWN, OP.add)
+            else:
+                act(pc("sf", k), sbank(k), AF.Identity, bias=0.0 if k < NS else -8 * DOWN, scale=8.0)
+            mm(w, A("g512"), pc("sf", k), False, True)
+            mm(u, A("s32"), pc("sf", k), k < NS, True)
+            if k < NS:
+                act(pc("sr", k), sbank(k), AF.Identity, bias=DOWN)
+
+        def ur(k):
+            act(pc("ur", k), bank(3, k), AF.Identity, bias=DOWN)
+            mm(A("ps7", 0, 128), A("ih"), pc("sr", k), True, False)
+            mm(A("ps7", 0, 128), A("nih"), pc("ur", k), False, True)
+
+        def r1(k):
+            act(pc("r1", k), A("ps7", 0, 128), AF.Relu)
+            u = bank(3, k)
+            mm(u, A("oneb", p1=1), A("kc", 0, 128, p1=1), True, False)
+            mm(u, A("ih"), pc("sr", k), False, False)
+            mm(u, A("nih"), pc("r1", k), False, True)
+
+        def low(k):
+            tt(own(kout, 2 * k, 2 * k + 2), bank(3, k), own(kin, 2 * k, 2 * k + 2), OP.min)
+
+        def x1(k):
+            tt(pc("x1", k), sbank(k), pc("a16", k), OP.min)
+
+        def scn(k):
+            scan(pc("scn", k), A("r64", 0, 128), bank(5, k), OP.min)
+
+        def x2(k):
+            tt(pc("x2", k), bank(3, k), pc("x1", k), OP.min)
+
+        def fin(k, on_v=False):
+            if on_v:
+                ts(own(kout, 2 * k, 2 * k + 2), pc("x2", k), -OFF, OP.add)
+            else:
+                act(own(kout, 2 * k, 2 * k + 2), pc("x2", k), AF.Identity, bias=-OFF)
+
+        def cvt(gi):
+            src = A("scn", 64 * GR[gi][0] + 63, 64 * GR[gi][1], 64)
+            if pas == 0:
+                cp(gc_("mi", gi, 1), src)
+            else:
+                tt(gc_("mi", gi, 1), src, gc_("f%d" % t, gi, 1), OP.min)
+
+        def band(gi):
+            ts(gc_("si%d" % t, gi, 1), gc_("mi", gi, 1), 511, OP.bitwise_and)
+
+        def u16(gi):
+            cp(gc_("su%d" % t, gi, 1), gc_("si%d" % t, gi, 1))
+
+        def out(gi):
+            cp(IND(own(kout, *GR[gi]), gc_("su%d" % t, gi, 1)), A("zero", 0, gn(gi, 16)))
+            send_group(kout, gi)
+
+        def sv(x0, x1_):
+            sg(x0, x1_); vg(x0, x1_)
+
+        sv(0, 16); sv(16, 32); sv(32, 64); ssum(0)
+        sv(64, 96); sg(96, 128); copy(0); vg(96, 128); ssum(1)
+        sg(128, 160); ur(0); vg(128, 160); scn(0); sg(160, 192); r1(0); copy(1); vg(160, 192); ssum(2)
+        sg(192, 224); ur(1); vg(192, 224); scn(1); low(0); sg(224, 256); r1(1); copy(2); vg(224, 256); ssum(3)
+        sg(256, 288); x1(2); scn(2); low(1); x2(2); vg(256, 288); copy(3); fin(2); sg(288, 320)
+        x1(3); scn(3); x2(3); cvt(0); fin(3, True); band(0); sg(320, 352)
+        vg(288, 304); u16(0); vg(304, 320); ssum(4); out(0); sg(352, 368); sg(368, 384)
+        vg(320, 352); copy(4); x1(4); vg(352, 368); scn(4); x2(4); fin(4); vg(368, 384); ssum(5)
+        copy(5); x1(5); scn(5); x2(5); cvt(1); fin(5, True); band(1); u16(1); out(1)
+
+    def prep_level(pas, t):
+        for gi in range(2):
+            su = gc_("su%d" % t, gi, 1)
+            cp(gc_("e%d" % t, gi, 16), IND(gc_("tri32", gi, 64), su))
+            act(gc_("c%d" % t, gi, 16), IND(gc_("phib", gi, 64), su))
+            if pas == 0:
+                act(gc_("ag%d" % t, gi, 16), IND(own(0, *GR[gi]), su))
+            else:
+                act(gc_("cf%d" % t, gi, 16), IND(gc_("phib", gi, 64), su))
+        if pas == 1:
+            scatter_const(lambda gi: gc_("lev", gi, 64), t, "l%d" % t)
+
+    def lists2(pas):
+        ts(A("j0"), A("si0"), 3, OP.bitwise_and)
+        ts(A("j1"), A("si1"), 3, OP.bitwise_and)
+        ts(A("b4"), A("si0"), 508, OP.bitwise_and)
+        tt(A("w0"), A("j0"), A("j1"), OP.mult)
+        tt(A("w1"), A("j0"), A("j1"), OP.add)
+        ts(A("w0"), A("w0"), 0.0, OP.is_equal)
+        ts(A("w2"), A("w1"), 1.0, OP.is_equal)
+        ts(A("w1"), A("w1"), -1.0, OP.mult, 6.0, OP.add)
+        tt(A("w0"), A("w0"), A("w2"), OP.add)
+        tt(A("w1"), A("w1"), A("b4"), OP.add)
+        tt(A("lo"), A("w0"), A("b4"), OP.add)
+        tt(A("hi"), A("w1"), A("w0"), OP.subtract)
+        cp(A("lou"), A("lo"))
+        cp(A("hiu"), A("hi"))
+        for src, dst in (("lou", "glo"), ("hiu", "ghi")):
+            for gi in range(2):
+                ts(gc_(dst, gi, 16), IND(gc_("tri32", gi, 64), gc_(src, gi, 1)), -1536.0, OP.add)
+        for bank, l0, l1 in (("ps0", "de", "do"), ("ps7", "se", "so")):
+            mm(A(bank, 0, 192), A(l0), A("glo"), True, False)
+            mm(A(bank, 0, 192), A(l1), A("ghi"), False, True)
+        if pas == 1:
+            tt(A("lop"), A("lo"), A("fx"), OP.max)
+            tt(A("hip"), A("hi"), A("fm"), OP.min)
+        ts(A("lx"), A("ps0", 0, 192), 1536.0, OP.add)
+        ts(A("ly"), A("ps7", 0, 192), 1536.0, OP.add)
+
+    def round2(pas, kin, kout):
+        tab = A("tab%d" % kin)
+        ext = arrived(kin)
+        lo, hi = ("lo", "hi") if pas == 0 else ("lop", "hip")
+
+        def sg(x0, x1):
+            act(A("ga", 16 * x0, 16 * x1), IND(tab, A("lx", x0, x1)), ext=ext)
+
+        def vg(x0, x1):
+            tt(A("mn", 16 * x0, 16 * x1), IND(tab, A("ly", x0, x1)), A("ga", 16 * x0, 16 * x1), OP.min, ext=ext)
+
+        def dsum(k):
+            gi = k // 2
+            o = A("ps%d" % (5 + gi), 64 * (k % 2), 64 * (k % 2) + 64)
+            mm(o, A("b1", p1=16), A("bd", 64 * k, 64 * k + 64, p1=16), True, False)
+            for e in range(2):
+                for m in range(8):
+                    mm(o, A("gp" if e == 0 else "gn"), A("mn", 1024 * k + 2 * m + e, 1024 * k + 1024, 16),
+                       False, e == 1 and m == 7)
+
+        def steps(gi):
+            n = gn(gi, 16)
+            y = gc_("y2", gi, 1)
+
+            def last():
+                cp(IND(own(kout, *GR[gi]), gc_("su2", gi, 1)), A("mark", 0, n))
+                send_group(kout, gi)
+            return [
+                lambda: scan(gc_("sc2", gi, 16), A("r16s", 0, n), A("ps%d" % (5 + gi), 0, n), OP.max),
+                lambda: tt(y, A("sc2", 16 * GR[gi][0] + 15, 16 * GR[gi][1], 16), gc_(lo, gi, 1), OP.max),
+                lambda: tt(gc_("si2", gi, 1), y, gc_(hi, gi, 1), OP.min),
+                lambda: cp(gc_("su2", gi, 1), gc_("si2", gi, 1)),
+                last]
+
+        sg(0, 16)
+        scatter_const(lambda gi: own(kout, *GR[gi]), 1, "mark")
+        vg(0, 16); sg(16, 32); vg(16, 32); sg(32, 48); vg(32, 48); sg(48, 64); vg(48, 64); dsum(0)
+        for x in range(64, 128, 16):
+            sg(x, x + 16); vg(x, x + 16)
+        dsum(1)
+        s0 = steps(0)
+        for i, x in enumerate(range(128, 192, 16)):
+            sg(x, x + 16); vg(x, x + 16)
+            if i == 3:
+                dsum(2)
+            s0[i]()
+        s0[4]()
+        for f in steps(1):
+            f()
+
+    def einit(t):
+        for k in range(3):
+            b = "ps%d" % k
+            mm(A(b), ONE33, K33("ke", 512), True, False)
+            for m in range(8):
+                mm(A(b, 64 * m, 64 * m + 64), A("nib"), A("c%d" % t, 64 * k, 64 * k + 64), False, False)
+
+    def level(pas, t, kin, kout):
+        tab = A("tab%d" % kin)
+        ext = arrived(kin)
+        need_p = not (pas == 0 and t == 0)
+        lst = "e%d" % t
+
+        def sg(x0, x1):
+            act(A("ga", 16 * x0, 16 * x1), IND(tab, A(lst, x0, x1)), ext=ext)
+
+        def vg(x0, x1):
+            cp(A("ga", 16 * x0, 16 * x1), IND(tab, A(lst, x0, x1)), ext=ext)
+
+        def esum(k):
+            for m in range(8):
+                for s in range(2):
+                    mm(A("ps%d" % k, 64 * m, 64 * m + 64), A("ib"), A("ga", 1024 * k + 2 * m + s, 1024 * k + 1024, 16),
+                       False, m == 7 and s == 1)
+
+        def part(n, k, m=None):
+            return A(n, 512 * k, 512 * k + 512) if m is None else A(n, 512 * k + 64 * m, 512 * k + 64 * m + 64)
+
+        def z(k):
+            act(part("zb", k), A("ps%d" % k), AF.Identity, bias=0.5)
+
+        def dif(k):
+            tt(part("db", k), A("ps%d" % k), part("zb", k), OP.subtract)
+            if need_p:
+                o = A("ps%d" % (3 + k // 2), 64 * (k % 2), 64 * (k % 2) + 64)
+                mm(o, ONE33, K33("kl", 64), True, False)
+                mm(o, A("ib"), A("c%d" % t, 64 * k, 64 * k + 64), False, False)
+                for m in range(8):
+                    mm(o, A("lu"), part("db", k, m), False, m == 7)
+
+        def thn(k):
+            ts(part("tb", k), part("zb", k), float(2 ** 20), OP.is_lt, A("thf"), OP.mult)
+
+        def absd(k):
+            act(part("ab", k), part("db", k), AF.Abs)
+            o = A("ps%d" % (5 + k // 2), 64 * (k % 2), 64 * (k % 2) + 64)
+            for m in range(8):
+                mm(o, A("gn"), part("tb", k, m), m == 0, False)
+            for m in range(8):
+                mm(o, A("gp"), part("ab", k, m), False, m == 7)
+
+        def zz(gi):
+            if need_p:
+                act(gc_("zz", gi, 16), A("ps%d" % (3 + gi), 0, gn(gi, 16)), AF.Identity, bias=-1663.5)
+
+        def phase(gi):
+            if need_p:
+                tt(gc_("rr", gi, 16), A("ps%d" % (3 + gi), 0, gn(gi, 16)), gc_("zz", gi, 16), OP.subtract)
+                ts(gc_("pb", gi, 16), gc_("rr", gi, 16), -1536.0, OP.add)
+
+        def post(gi):
+            if t > 0:
+                ts(gc_("mk", gi, 16), A("ps%d" % (5 + gi), 0, gn(gi, 16)), 0.0, OP.is_gt, MARK, OP.mult)
+                tt(IND(own(kout, *GR[gi]), gc_("su%d" % t, gi, 1)), gc_("pb", gi, 16), gc_("mk", gi, 16), OP.add)
+            else:
+                record(gi)
+            if t > 0 or pas == 0:
+                send_group(kout, gi)
+            else:
+                c0, c1 = 64 * GR[gi][0], 64 * GR[gi][1]
+                store(T.yphi[:, c0:c1], A("pout", c0, c1), "d_y%d" % gi)
+
+        def record(gi):
+            su = gc_("su%d" % t, gi, 1)
+            if pas == 1:
+                tt(gc_("dd", gi, 16), gc_("pb", gi, 16), gc_("c%d" % t, gi, 16), OP.subtract)
+            ts(gc_("nk", gi, 16), A("ps%d" % (5 + gi), 0, gn(gi, 16)), 0.0, OP.is_le)
+            if pas == 0:
+                tt(IND(own(6, *GR[gi]), su), gc_("ag%d" % t, gi, 16), gc_("nk", gi, 16), OP.mult)
+            else:
+                tt(gc_("tt", gi, 16), gc_("dd", gi, 16), gc_("nk", gi, 16), OP.mult)
+                tt(IND(gc_("pout", gi, 64), su), gc_("tt", gi, 16), gc_("cf%d" % t, gi, 16), OP.add)
+
+        sg(0, 32); vg(32, 64); esum(0)
+        sg(64, 96); vg(96, 128); esum(1)
+        z(0); vg(160, 192); sg(128, 160); dif(0); thn(0); esum(2)
+        z(1); absd(0); dif(1); thn(1)
+        z(2); absd(1); zz(0); dif(2); thn(2); absd(2)
+        phase(0); post(0); zz(1); phase(1); post(1)
+        if t > 0:
+            if t == 2:
+                act(own(kout + 1), own(kout))
+            record(0); record(1)
+        if pas == 0:
+            mm(A("ps7", 0, 192), A("b1", p1=16), A("bd", p1=16), True, False)
+            mm(A("ps7", 0, 192), A("ib"), A("nk"), False, True)
+            scan(A("sc2"), A("r16s"), A("ps7", 0, 192), OP.max)
+            ts(A("w3"), A("sc2", 15, 192, 16), float(2 ** 26), OP.mult, -512.0, OP.add)
+            tt(A("k%d" % t), A("w3"), A("si%d" % t), OP.add)
+
+    def forced():
+        tt(A("w0"), A("k0"), A("k1"), OP.min)
+        tt(A("w1"), A("k0"), A("k1"), OP.max)
+        tt(A("f0"), A("w0"), A("k2"), OP.min)
+        tt(A("w2"), A("w1"), A("k2"), OP.min)
+        tt(A("w1"), A("w1"), A("k2"), OP.max)
+        tt(A("f1"), A("w0"), A("w2"), OP.max)
+        ts(A("fm"), A("w1"), 512.0, OP.add)
+        ts(A("w3"), A("w1"), 1000.0, OP.is_gt, -float(2 ** 27), OP.mult)
+        tt(A("fx"), A("fm"), A("w3"), OP.add)
+
+    for pas in range(2):
+        k = 6 * pas
+        if pas == 1:
+            forced()
+            prep_a16(k)
+        round01(pas, 0, k, k + 1)
+        prep_a16(k + 1)
+        act(own(k + 3), A("phib"))
+        scatter_const(lambda gi: gc_("dp%d" % pas, gi, 64), 0, "big")
+        prep_level(pas, 0)
+        scatter_const(lambda gi: own(k + 3, *GR[gi]), 0, "mark")
+        round01(pas, 1, k + 1, k + 2)
+        lists2(pas)
+        round2(pas, k + 2, k + 3)
+        prep_level(pas, 2)
+        einit(2)
+        act(own(k + 4), own(k + 3))
+        prep_level(pas, 1)
+        if pas == 0:
+            act(own(6), own(0))
+        else:
+            rec("s", lambda: g.sync.dma_start(T.ylev[:], T.lev[0:128:16, :]), [], [A("lev")], sem="d_lev")
+        level(pas, 2, k + 3, k + 4)
+        einit(1)
+        if pas == 0:
+            ms(A("dp1"), 0.0)
+            ms(A("lev"), 3.0)
+            for i in range(3):
+                ms(A("l%d" % i), float(i))
+        level(pas, 1, k + 4, k + 5)
+        einit(0)
+        if pas == 0:
+            act(A("pout"), A("phib"))
+        level(pas, 0, k + 5, k + 6)
+
+    hist, seq = {}, {}
+    known = {q: {} for q in "vapgs"}
+    for i, o in enumerate(ops):
+        q = o["q"]
+        deps = set()
+        touched = [(d, False) for d in o["rd"]] + [(d, True) for d in o["wr"]]
+        for d, w in touched:
+            h = hist.setdefault(d[0], [])
+            if d[0].startswith("ps"):
+                for (lo_, hi_, j, jw) in h:
+                    if ops[j]["q"] != q or (q != "p" and (w or jw)):
+                        deps.add(j)
+            else:
+                for (lo_, hi_, j, jw) in h:
+                    if (w or jw) and lo_ < d[2] and d[1] < hi_:
+                        deps.add(j)
+        deps.discard(i)
+        for d, w in touched:
+            h = hist[d[0]]
+            if d[0].startswith("ps"):
+                h[:] = [e for e in h if ops[e[2]]["q"] != q or (e[3] and not w)]
+            elif w and d[3] == 1 and d[4] == 0 and d[5] == 128:
+                h[:] = [e for e in h if not (d[1] <= e[0] and e[1] <= d[2])]
+            elif not w:
+                h[:] = [e for e in h if e[3] or ops[e[2]]["q"] != q or ops[e[2]]["sem"]
+                        or not (d[1] <= e[0] and e[1] <= d[2])]
+            h.append((d[1], d[2], i, w))
+        kn = known[q]
+        waits = []
+        if o["ext"] and kn.get(o["ext"][0], 0) < o["ext"][1]:
+            waits.append(o["ext"])
+            kn[o["ext"][0]] = o["ext"][1]
+        for j in sorted(deps, reverse=True):
+            key, val = ops[j]["done"]
+            if kn.get(key, 0) >= val:
+                continue
+            waits.append(j)
+            ops[j]["need"] = True
+            for k2, v2 in ops[j]["clock"].items():
+                if kn.get(k2, 0) < v2:
+                    kn[k2] = v2
+            kn[key] = val
+        o["waits"] = waits
+        o["clock"] = dict(kn)
+        key = o["sem"] or q
+        seq[key] = seq.get(key, 0) + (16 if o["sem"] else 1)
+        o["done"] = (key, seq[key])
+    eng = {"v": g.vector, "a": g.scalar, "p": g.tensor, "g": g, "s": g.sync}
+    cnt = {}
+    for o in ops:
+        q = o["q"]
+        for w in o["waits"]:
+            s, v = w if isinstance(w, tuple) else ops[w]["sig"]
+            eng[q].wait_ge(T.sem[s], v)
+        ins = o["fn"]()
+        if o["sem"] == "none":
+            continue
+        if o["sem"]:
+            ins.then_inc(T.sem[o["sem"]], 16)
+            o["sig"] = o["done"]
+        elif o.get("need"):
+            cnt[QSEM[q]] = cnt.get(QSEM[q], 0) + 1
+            ins.then_inc(T.sem[QSEM[q]], 1)
+            o["sig"] = (QSEM[q], cnt[QSEM[q]])
+    g.wait_ge(T.sem.sent, nsent[0])
+    for s in ("d_lev", "d_y0", "d_y1"):
+        g.sync.wait_ge(T.sem[s], 16)

@@ -3,8 +3,21 @@ from concourse.mybir import AluOpType, ActivationFunctionType
 
 NV, NW = 768, 3072
 GR = [(0, 8), (8, 12)]
-NS = 2
-TWO = (1, 2, 7, 8)
+FIRST = [(0, 6), (6, 12)]
+SR = [(0, 4), (4, 8), (8, 12)]
+EARLY = 0.5
+ROOM = 3.2
+S2 = [(0, 8), (8, 12)]
+SL = [(0, 12)]
+RP = [(0, 2), (2, 4), (4, 6), (6, 8), (8, 10), (10, 11), (11, 12)]
+R2 = [(0, 4), (4, 8), (8, 11), (11, 12)]
+LP = [(0, 4, [(0, 0, 8)]), (4, 8, [(1, 0, 8)]), (8, 12, [(2, 0, 4), (7, 4, 8)])]
+LG = "aavvaavvavvv"
+LO = "f0 f1 z0 f2 z1 d0 z20 d1 z21 a0 l0 d20 a1 l1 d21 s0 s1 a20 l20 a21 l21 s20 s21"
+TG = "avaava"
+NEAR = 4
+THS = ()
+ABS = (0, 1, 2)
 OFF = 1088.0
 MARK = float(2 ** 42)
 BF, F16, F32, I32, U16 = "bfloat16", "float16", "float32", "int32", "uint16"
@@ -18,48 +31,51 @@ def _sb(dt, cols, names):
         SCRATCH[n] = ("sbuf", [128, cols], dt)
 
 
-def _pack(base, dt, names):
+def _pack(base, dt, cols, names):
+    step = max(cols, 16)
     for i, n in enumerate(names.split()):
-        PART[n] = (base, 16 * i)
-    _sb(dt, 16 * len(names.split()), base)
+        PART[n] = (base, step * i, cols)
+    _sb(dt, step * len(names.split()), base)
 
 
-_sb(I32, NV, "amp32 phi32 tri32")
+_sb(I32, NV, "amp32 phi32 tri32 tq32")
 _sb(I32, 1, "th32")
 _sb(F32, 1, "thf")
-_sb(BF, NW, " ".join("tab%d" % i for i in range(12)))
+_sb(BF, NW, "tab0 tab1 tab2 tab3 tab6 tab7 tab8 tab9")
+_sb(BF, NW + NV, "tab4 tab10")
 _sb(BF, 6144, "ga mn")
 _sb(BF, 1536, "zb db ab tb")
 _sb(U16, 384, "offa offb")
-_sb(U16, 192, "lx ly e0 e1 e2")
-_sb(F16, NV, "r16 a16 x1 x2 sf sr ur r1")
+_pack("l192", U16, 192, "lx ly e0 e1 e2 f0")
+_sb(F16, NV, "r16 x1 xa xb sf")
 _sb(F32, NV, "scn pout lev")
-_sb(BF, NV, "phib dp0 dp1")
-_sb(F16, 192, "glo ghi rr")
-_sb(BF, 192, "bd c0 c1 c2 ag0 ag1 ag2 zz pb mk nk dd")
-_sb(F32, 192, "cf0 cf1 cf2 tt r16s sc2")
-_sb(F32, 512, "r64")
-_sb(BF, 512, "ke kc")
-_sb(BF, 128, "oneb moneb eight ib nib i8 gt gp gn b1 lu s64 ks kl zero mark big")
-_sb(F16, 128, "de do se so b512 bh g512 s32 ih nih")
-_sb(F32, 128, "l0 l1 l2 bhi bhs")
-_pack("smi", I32, "mi si0 si1 si2 j0 j1 b4")
-_pack("smu", U16, "su0 su1 su2 lou hiu")
-_pack("smf", F32, "w0 w1 w2 w3 lo hi lop hip k0 k1 k2 f0 f1 fm fx y2")
+_sb(BF, NV, "phib fl0 fl1 ck")
+_pack("h192", F16, 192, "glo ghi rr")
+_pack("b192", BF, 192, "c0 c1 c2 ag0 jv0 jv1 jv2 cl ch zz pb mk nk dd bd kq")
+_pack("f192", F32, 192, "cf0 cf1 cf2 cq0 cq1 tt r16s sc2 qa kf")
+_sb(F32, 128, "r64 l2")
+_sb(BF, 512, "ke kn kv jc pick")
+_sb(BF, 2048, "dm")
+_pack("b128", BF, 128, "oneb ib nib i8 i20 i1k ni1k gt gp gn xp xp2 xn g1n g512 g3 g2 gm gm2 b1 lu s64 ks ku kl kb kx mark")
+_pack("h128", F16, 128, "p00 p01 p10 p11 gh s32")
+_pack("smi", I32, 12, "mi si0 si1 si2 j0 j1 io0 io1")
+_pack("smu", U16, 12, "su0 su1 su2 lou hiu")
+_pack("smf", F32, 12, "w0 w1 w2 lo hi y2 base")
 for _i in range(8):
     SCRATCH["ps%d" % _i] = ("psum", [128, 512], F32)
 
-SEMAPHORES = (["sv", "sa", "sp", "sg", "sent", "d_amp", "d_tri", "d_phi", "d_th", "d_y0", "d_y1", "d_lev"]
+SEMAPHORES = (["sv", "sa", "sp", "sg", "sent", "d_a0", "d_a1", "d_tri", "d_phi", "d_th", "d_y0", "d_y1", "d_lev"]
               + ["arr%d" % i for i in range(12)])
 QSEM = {"v": "sv", "a": "sa", "p": "sp", "g": "sg"}
 OP = AluOpType
 AF = ActivationFunctionType
+CYC, GAT, SCA, PEC, HOP, LAT, ROW, BYTE = 0.0009, 1.56, 3.8, 0.0005, 0.1, 2.5, 0.045, 0.00005
 
 
 def A(name, c0=0, c1=None, step=1, p0=0, p1=128):
     if name in PART:
-        base, o = PART[name]
-        return (base, o + c0, o + (12 if c1 is None else c1), step, p0, p1)
+        base, o, cols = PART[name]
+        return (base, o + c0, o + (cols if c1 is None else c1), step, p0, p1)
     if c1 is None:
         c1 = SCRATCH[name][1][1]
     return (name, c0, c1, step, p0, p1)
@@ -69,11 +85,20 @@ def IND(win, off):
     return ("*", win, off)
 
 
+def width(d):
+    return 16 * (d[2][2] - d[2][1]) if d[0] == "*" else (d[2] - d[1] + d[3] - 1) // d[3]
+
+
+def narrow(*ds):
+    return all(SCRATCH[d[0]][2] in (BF, F16, U16) for d in ds)
+
+
 def rank_program(g, core, T, topo):
     rank = T.rank_of(core)
     if rank is None:
         return
     ops = []
+    now = {"step": -1, "side": None}
 
     def ap(d):
         if not isinstance(d, tuple):
@@ -86,7 +111,7 @@ def rank_program(g, core, T, topo):
             return t[:, c0:c1] if st == 1 else t[:, c0:c1:st]
         return t[p0:p1, c0:c1] if st == 1 else t[p0:p1, c0:c1:st]
 
-    def rec(q, fn, outs, ins, ext=None, sem=None):
+    def rec(q, fn, outs, ins, cost, ext=None, sem=None, lag=HOP):
         rd, wr = [], []
         for d in outs:
             if d[0] == "*":
@@ -99,59 +124,73 @@ def rank_program(g, core, T, topo):
                     rd.append(d[1]); rd.append(d[2])
                 else:
                     rd.append(d)
-        ops.append({"q": q, "fn": fn, "rd": rd, "wr": wr, "ext": ext, "sem": sem})
+        ops.append({"q": q, "fn": fn, "rd": rd, "wr": wr, "ext": ext, "sem": sem, "cost": cost, "lag": lag, **now})
+
+    def dur(o, i, per=None):
+        if i is not None and i[0] == "*":
+            return 0.06 + GAT * CYC * width(i)
+        if o[0] == "*":
+            return 0.05 + SCA * CYC * width(o)
+        if per is None:
+            per = 0.5 if narrow(o, i or o) else 1.0
+        return CYC * max(64, per * width(o))
 
     def cp(o, i, ext=None):
-        rec("v", lambda: g.vector.tensor_copy(ap(o), ap(i)), [o], [i], ext)
+        rec("v", lambda: g.vector.tensor_copy(ap(o), ap(i)), [o], [i], dur(o, i), ext)
 
     def tt(o, a, b, op, ext=None):
-        rec("v", lambda: g.vector.tensor_tensor(ap(o), ap(a), ap(b), op), [o], [a, b], ext)
+        per = 1.0 if a[0].startswith("ps") else 2.0
+        rec("v", lambda: g.vector.tensor_tensor(ap(o), ap(a), ap(b), op), [o], [a, b], dur(o, a, per), ext)
 
     def ts(o, a, s1, op0, s2=None, op1=None):
         if op1 is None:
-            rec("v", lambda: g.vector.tensor_scalar(ap(o), ap(a), ap(s1), None, op0), [o], [a, s1])
+            rec("v", lambda: g.vector.tensor_scalar(ap(o), ap(a), ap(s1), None, op0), [o], [a, s1], dur(o, a))
         else:
-            rec("v", lambda: g.vector.tensor_scalar(ap(o), ap(a), ap(s1), ap(s2), op0, op1), [o], [a, s1, s2])
+            rec("v", lambda: g.vector.tensor_scalar(ap(o), ap(a), ap(s1), ap(s2), op0, op1), [o], [a, s1, s2], dur(o, a))
 
     def ms(o, val):
-        rec("v", lambda: g.vector.memset(ap(o), val), [o], [])
+        rec("v", lambda: g.vector.memset(ap(o), val), [o], [], dur(o, None))
 
     def scan(o, d0, d1, op1):
-        rec("v", lambda: g.vector.tensor_tensor_scan(ap(o), ap(d0), ap(d1), 0.0, OP.add, op1), [o], [d0, d1])
+        rec("v", lambda: g.vector.tensor_tensor_scan(ap(o), ap(d0), ap(d1), 0.0, OP.add, op1), [o], [d0, d1], dur(o, d1))
 
     def act(o, i, func=AF.Copy, bias=0.0, scale=1.0, ext=None):
-        rec("a", lambda: g.scalar.activation(ap(o), ap(i), func, bias=bias, scale=scale), [o], [i], ext)
+        rec("a", lambda: g.scalar.activation(ap(o), ap(i), func, bias=ap(bias), scale=scale), [o], [i, bias],
+            dur(o, i, 1.0), ext)
 
     def mm(o, l, r, start, stop):
-        rec("p", lambda: g.tensor.matmul(ap(o), ap(l), ap(r), start, stop), [o], [l, r])
+        rec("p", lambda: g.tensor.matmul(ap(o), ap(l), ap(r), start, stop), [o], [l, r], PEC * max(64, width(r)))
 
     def sel(o, i, pat, cmp, fill, base, cm):
-        rec("g", lambda: g.affine_select(ap(o), ap(i), pat, cmp, fill, base, cm), [o], [i])
+        rec("g", lambda: g.affine_select(ap(o), ap(i), pat, cmp, fill, base, cm), [o], [i], 0.17 + 2 * CYC * width(o))
 
-    def load(o, src, sem):
-        rec("s", lambda: g.sync.dma_start(ap(o), src), [o], [], sem=sem)
+    def iota(o, pat, base, cm):
+        rec("g", lambda: g.iota(ap(o), pat, base, cm), [o], [], 0.13 + 2 * CYC * width(o))
+
+    def load(q, o, src, sem):
+        e = g.sync if q == "s" else g.scalar
+        rec(q, lambda: e.dma_start(ap(o), src), [o], [], 0.1, sem=sem, lag=LAT + 32 * BYTE * width(o))
 
     def store(dst, i, sem):
-        rec("s", lambda: g.sync.dma_start(dst, ap(i)), [], [i], sem=sem)
+        rec("s", lambda: g.sync.dma_start(dst, ap(i)), [], [i], 0.1, sem=sem, lag=LAT)
 
     peers = [c for c in T.cores if c != core]
     near = [c for c in peers if c in topo.cores_of(core)]
     far = [c for c in peers if c not in near]
     off_eng = topo.engines(core, far[0])
     on_eng = [e for e in topo.engines(core, near[0]) if e not in off_eng]
+    on_eng = on_eng[::len(on_eng) // NEAR]
     share = len(off_eng) // len(far)
     masks = {near[0]: sum(1 << e for e in on_eng)}
     for i, c in enumerate(far):
         masks[c] = sum(1 << e for e in off_eng[i * share:(i + 1) * share])
     per_send = len(on_eng) + share * len(far)
-    nsent = [0]
+    sends = {}
 
-    def own(k, c0=0, c1=12):
-        return A("tab%d" % k, rank * NV + 64 * c0, rank * NV + 64 * c1)
+    def own(k, u0=0, u1=12):
+        return A("tab%d" % k, rank * NV + 64 * u0, rank * NV + 64 * u1)
 
-    def send(k, c0=0, c1=12):
-        d = own(k, c0, c1)
-
+    def send(k, d):
         def fn():
             trs = []
             for c in far + near:
@@ -159,479 +198,527 @@ def rank_program(g, core, T, topo):
                 trs.append(RemoteDMATransfer(dst_ids=[DstId(rid=rid, pnc=pid)], dma_engine_mask=masks[c],
                                              remote_sem=T.sem["arr%d" % k], src=ap(d), dst=ap(d)))
             g.remote_dma_fused(trs, local_sem=T.sem.sent)
-        nsent[0] += per_send
-        rec("g", fn, [], [d], sem="none")
+        sends.setdefault(k, []).append(len(ops))
+        rec("g", fn, [], [d], 0.3, sem="none", lag=128 // share * (ROW + 2 * BYTE * width(d)))
 
-    def send_group(k, gi):
-        if k in TWO:
-            send(k, *GR[gi])
-        elif gi == 1:
-            send(k)
+    def send_done(k, u1, parts):
+        for a, b in parts:
+            if b == u1:
+                send(k, own(k, a, b))
 
-    def arrived(k):
-        return ("arr%d" % k, per_send * (len(GR) if k in TWO else 1))
+    def U(name, u0, u1, per):
+        return A(name, per * u0, per * u1)
 
-    def gc_(name, gi, per):
-        return A(name, per * GR[gi][0], per * GR[gi][1])
+    def G(name, gi, per):
+        return U(name, GR[gi][0], GR[gi][1], per)
 
-    def gn(gi, per):
-        return per * (GR[gi][1] - GR[gi][0])
+    def group(u):
+        return [gi for gi, (a, b) in enumerate(GR) if a <= u < b][0]
 
-    def scatter_const(win, t, src):
-        for gi in range(2):
-            cp(IND(win(gi), gc_("su%d" % t, gi, 1)), A(src, 0, gn(gi, 16)))
+    def ends(u1):
+        return [gi for gi, (a, b) in enumerate(GR) if b == u1]
 
-    load(A("amp32"), T.amp[:], "d_amp")
-    load(A("tri32"), T.tri[:], "d_tri")
-    load(A("phi32"), T.phi[:], "d_phi")
-    load(A("th32"), T.th[:], "d_th")
+    GI = range(len(GR))
+    ONE33, ONE1 = A("oneb", p1=33), A("oneb", p1=1)
+    B16 = A("b1", p1=16)
+    DOWN = OFF - 31.0 / 64
+
+    for i, (u0, u1) in enumerate(FIRST):
+        load("sa"[i], U("amp32", u0, u1, 64), T.amp[:, 64 * u0:64 * u1], "d_a%d" % i)
+    load("s", A("tri32"), T.tri[:], "d_tri")
+    load("s", A("phi32"), T.phi[:], "d_phi")
+    load("s", A("th32"), T.th[:], "d_th")
+    for u0, u1 in FIRST:
+        cp(own(0, u0, u1), U("amp32", u0, u1, 64))
+    send(0, own(0))
+    now.update(side=-1)
     ms(A("oneb"), 1.0)
-    ms(A("eight"), 0.125)
-    picks = (("de", 200, 0), ("do", -200, 199), ("se", 200, -1), ("so", -200, 200))
-    for i, (n, st, base) in enumerate(picks):
-        sel(A("mn", 128 * i, 128 * i + 128), A("oneb"), [[-2, 64], [st, 2]], OP.is_equal, 0.0, base, 1)
-    sel(A("i8"), A("eight"), [[-1, 128]], OP.is_equal, 0.0, 0, 1)
-    sel(A("b1", p1=16), A("oneb", p1=16), [[0, 8], [-1, 16]], OP.is_equal, 0.0, 0, 1)
-    ms(A("moneb"), -1.0)
-    rows = (("ks", OFF, -31.0 / 64), ("kl", 50688.0, -63.0 / 128))
-    for n, a, b in rows:
-        ms(A(n, p1=64), 0.0)
-    ms(A("ke", p1=64), 0.0)
-    ms(A("zero"), 0.0)
-    ms(A("bd", p1=32), 0.0)
-    ms(A("r64"), 0.0)
-    ms(A("r16s"), 0.0)
-    for n, a, b in rows:
-        ms(A(n, p1=1), a)
-        ms(A(n, p0=32, p1=33), b)
-    ms(A("ke", p1=1), 49152.0)
-    ms(A("r64", 0, 512, 64), float(2 ** 26))
-    ms(A("r16s", 0, 192, 16), -float(2 ** 28))
-    ms(A("kc", 0, 128, p1=1), -OFF)
-    for i in range(1, 4):
-        ms(A("kc", 128 * i, 128 * i + 128, p1=1), 128.0 * i)
-    ms(A("mark"), MARK)
-    ms(A("big"), float(2 ** 25))
-    for i, (n, st, base) in enumerate(picks):
-        cp(A(n), A("mn", 128 * i, 128 * i + 128))
-    cp(own(0), A("amp32"))
-    send(0)
-    ts(A("r16"), A("tri32"), -1536.0, OP.add)
+    for s in range(2):
+        for e in range(2):
+            o = A("pick", 256 * s + 128 * e, 256 * s + 128 * e + 128)
+            sel(o, A("oneb"), [[-16, 8], [200 - 400 * e, 2], [-2, 8]], OP.is_equal, 0.0, 200 * e - s, 1)
+            cp(A("p%d%d" % (s, e)), o)
     sel(A("ib"), A("oneb"), [[-1, 128]], OP.is_equal, 0.0, 0, 1)
-    sel(A("nib"), A("moneb"), [[-1, 128]], OP.is_equal, 0.0, 0, 1)
+    sel(B16, A("oneb", p1=16), [[0, 8], [-1, 16]], OP.is_equal, 0.0, 0, 1)
     sel(A("gt"), A("oneb"), [[-16, 8], [0, 16]], OP.is_ge, 0.0, 0, 1)
     sel(A("gt"), A("gt"), [[16, 8], [0, 16]], OP.is_ge, 0.0, 15, -1)
-    rec("g", lambda: g.iota(ap(A("bhi", p1=16)), [[1, 128]], 0, 0, allow_small_or_imprecise_dtypes=True),
-        [A("bhi", p1=16)], [])
-    sel(A("bhs", p1=16), A("bhi", p1=16), [[0, 2], [-1, 16], [0, 4]], OP.is_equal, 60000.0 * 512, 0, 1)
-    sel(A("bd", p1=16), A("bd", p1=16), [[0, 12], [-1, 16]], OP.is_equal, -float(2 ** 27), 0, 1)
-    for bank, l0, l1 in (("ps6", "de", "do"), ("ps7", "se", "so")):
-        for k in range(6):
-            mm(A(bank, 64 * k, 64 * k + 64), A(l0), A("r16", 128 * k, 128 * k + 64), True, False)
-            mm(A(bank, 64 * k, 64 * k + 64), A(l1), A("r16", 128 * k + 64, 128 * k + 128), False, True)
-    mm(A("ps5", 0, 128), A("b1", p1=16), A("b1", p1=16), True, True)
-
-    def prep_a16(k):
-        act(A("a16", 128 * NS, NV), own(k, 2 * NS, 12), AF.Identity, bias=OFF)
-
-    prep_a16(0)
-    ts(A("offa"), A("ps6", 0, 384), 1536.0, OP.add)
-    ts(A("offb"), A("ps7", 0, 384), 1536.0, OP.add)
+    for j in range(4):
+        ms(A("kb", j, 128, 4, p1=16), -j / 4.0)
+        ms(A("jc", j, 512, 4), (j - 4) * 2.0 ** 16 / MARK)
+    sel(A("kb", p1=16), A("kb", p1=16), [[0, 2], [-1, 16], [0, 4]], OP.is_equal, -float(2 ** 22), 0, 1)
+    ms(A("bd", p1=16), 0.0)
+    sel(A("bd", p1=16), A("bd", p1=16), [[0, 12], [-1, 16]], OP.is_equal, -2 * MARK, 0, 1)
+    iota(A("io0"), [[0, 12]], 0, 4)
+    for gi in GI:
+        iota(G("io1", gi, 1), [[64, GR[gi][1] - GR[gi][0]]], 0, 0)
+    ts(A("io0"), A("io0"), 63, OP.bitwise_and)
+    tt(A("base"), A("io0"), A("io1"), OP.add)
+    for n, a, b in (("ks", OFF, -31.0 / 64), ("ku", OFF - 8192, -31.0 / 64), ("kl", 50688.0, -63.0 / 128)):
+        ms(A(n, p1=64), 0.0)
+        ms(A(n, p1=1), a)
+        ms(A(n, p0=32, p1=33), b)
+    for n, a in (("ke", 49152.0), ("kv", -77.0), ("kn", 48 * MARK), ("kx", -2 * MARK), ("kq", -4096.0)):
+        ms(A(n, p1=1), a)
+    ms(A("r64"), 0.0)
+    ms(A("r64", 0, 128, 64), -float(2 ** 26))
+    ms(A("r16s"), 0.0)
+    ms(A("r16s", 0, 192, 16), -4 * MARK)
+    ms(A("l2"), 2.0)
+    ms(A("ck"), 0.0)
+    ts(A("r16"), A("tri32"), -1536.0, OP.add)
+    for s, dst in enumerate(("offa", "offb")):
+        for e in range(2):
+            mm(A("ps%d" % (6 + s), 0, 384), A("p%d%d" % (s, e)), A("r16", e, NV, 2), e == 0, e == 1)
+        ts(A(dst), A("ps%d" % (6 + s), 0, 384), 1536.0, OP.add)
+    mm(A("ps5", 0, 128), B16, B16, True, True)
     ts(A("s32"), A("ps5", 0, 128), 1.0 / 32, OP.mult)
     ts(A("s64"), A("ps5", 0, 128), 1.0 / 64, OP.mult)
-    ts(A("b512", p1=16), A("b1", p1=16), 512.0, OP.mult)
+    for n, f in (("i8", 0.125), ("nib", -1.0), ("i20", 2.0 ** 20), ("i1k", 1024.0), ("ni1k", -1024.0)):
+        ts(A(n), A("ib"), f, OP.mult)
+    for n, f in (("gh", -1.0), ("g1n", -1.0), ("g512", 512.0), ("gp", 1024.0), ("gn", -1024.0), ("xp", 4 * MARK),
+                 ("xp2", 8 * MARK), ("xn", -4 * MARK), ("gm", -MARK), ("gm2", -2 * MARK), ("g3", 3.0), ("g2", 2.0)):
+        ts(A(n), A("gt"), f, OP.mult)
+    tt(A("lu"), A("s64"), A("i8"), OP.add)
     cp(A("phib"), A("phi32"))
     cp(A("thf"), A("th32"))
-    ms(A("dp0"), 0.0)
-    tt(A("lu"), A("s64"), A("i8"), OP.add)
-    cp(A("ih"), A("ib"))
-    cp(A("nih"), A("nib"))
-    ts(A("g512"), A("gt"), 512.0, OP.mult)
-    ts(A("gp"), A("gt"), 1024.0, OP.mult)
-    ts(A("gn"), A("gt"), -1024.0, OP.mult)
-    ts(A("bh", p1=16), A("bhs", p1=16), 1.0 / 512, OP.mult)
+    ts(A("tq32"), A("tri32"), 2, OP.arith_shift_right)
+    for r in range(16):
+        ts(A("dm", 128 * r, 128 * r + 128), A("ib"), A("s64", r, r + 1), OP.mult, 64 * 4096 / MARK, OP.mult)
+    ms(A("mark"), MARK)
+    act(A("pout"), A("phib"))
 
-    def K33(n, w):
-        return A(n, 0, w, p1=33)
-    ONE33 = A("oneb", p1=33)
-    DOWN = OFF - 31.0 / 64
+    def pair_gathers(tab, k, la, lb, cuts):
+        for x0, x1 in zip(cuts[:-1], cuts[1:]):
+            act(A("ga", 16 * x0, 16 * x1), IND(tab, A(la, x0, x1)), ext=k)
+            tt(A("mn", 16 * x0, 16 * x1), IND(tab, A(lb, x0, x1)), A("ga", 16 * x0, 16 * x1), OP.min, ext=k)
 
     def round01(pas, t, kin, kout):
         tab = A("tab%d" % kin)
-        ext = arrived(kin)
+        ain, aout = ("xb", "xa") if t == 0 else ("xa", "xb")
+        fl = "fl%d" % t
+        now.update(step=kin, side=kin)
+        if t == 0:
+            act(A(ain), own(kin), AF.Identity, bias=OFF)
+        now.update(side=None)
+        for i, (u0, u1) in enumerate(RP):
+            w = 64 * (u1 - u0)
+            last = u1 == 12
+            cuts = list(range(32 * u0, 32 * u1 + 1, 32))
+            if u0 == 0:
+                cuts.insert(1, 8)
+            if last:
+                cuts.insert(-1, cuts[-1] - 12)
+            pair_gathers(tab, kin, "offa", "offb", cuts)
+            sb, kb, ub = (A("ps%d" % b, 0, w) for b in (i % 3, 3 + i % 2, 5 + i % 3))
 
-        def sg(x0, x1):
-            act(A("ga", 16 * x0, 16 * x1), IND(tab, A("offa", x0, x1)), ext=ext)
+            def pc(n):
+                return U(n, u0, u1, 64)
 
-        def vg(x0, x1):
-            tt(A("mn", 16 * x0, 16 * x1), IND(tab, A("offb", x0, x1)), A("ga", 16 * x0, 16 * x1), OP.min, ext=ext)
-
-        def pc(n, k, k1=None):
-            return A(n, 128 * k, 128 * (k + 1 if k1 is None else k1))
-
-        def sbank(k):
-            return A("ps%d" % (k % 3), 0, 128)
-
-        def bank(first, k):
-            gi = 0 if 2 * k < GR[0][1] else 1
-            o = 128 * k - 64 * GR[gi][0]
-            return A("ps%d" % (first + gi), o, o + 128)
-
-        def ssum(k):
-            b = "ps%d" % (k % 3)
-            if k >= NS:
-                mm(sbank(k), ONE33, K33("ks", 128), True, False)
-            for e in range(2):
-                for m in range(8):
-                    mm(A(b, 64 * e, 64 * e + 64), A("i8"), A("mn", 1024 * k + 2 * m + e, 1024 * k + 1024, 16),
-                       k < NS and m == 0, m == 7 and (k < NS or e == 1))
-
-        def copy(k):
-            w, u = bank(5, k), bank(3, k)
-            mm(w, A("b512", p1=16), A("bh", p1=16), True, False)
-            if w[1]:
-                mm(w, A("oneb", p1=1), A("kc", w[1], w[2], p1=1), False, False)
+            def trip(m):
+                return A("mn", 512 * u0 + m, 512 * u1, 8)
+            mm(kb, B16, A("kb", 0, w, p1=16), True, False)
             if t == 1:
-                mm(w, A("ib"), pc("dp%d" % pas, k), False, False)
-            if k >= NS:
-                mm(u, ONE33, K33("ks", 128), True, False)
-            if k == 5:
-                ts(pc("sf", k), sbank(k), 8.0, OP.mult, -8 * DOWN, OP.add)
+                mm(kb, A("i20"), pc("fl0"), False, False)
+            if pas == 1:
+                mm(kb, A("nib"), pc("ck"), False, False)
+            if last:
+                for m in range(8):
+                    mm(kb, A("g1n"), trip(m), False, m == 7)
+            mm(sb, ONE33, A("ks", 0, w, p1=33), True, False)
+            for m in range(8):
+                mm(sb, A("i8"), trip(m), False, m == 7)
+            act(pc("sf"), sb, AF.Identity, bias=-8 * DOWN, scale=8.0)
+            tt(pc("x1"), sb, pc(ain), OP.min)
+            if not last:
+                mm(kb, A("gh"), pc("sf"), False, True)
+            mm(ub, ONE33, A("ku", 0, w, p1=33), True, False)
+            mm(ub, A("s32"), pc("sf"), False, False)
+            scan(pc("scn"), A("r64", 0, w), kb, OP.max)
+            for u in range(u0, u1):
+                act(U(fl, u, u + 1, 64), A(kb[0], 64 * (u - u0), 64 * (u - u0) + 64), AF.Sign, scale=-1.0,
+                    bias=A("scn", 64 * u + 63, 64 * u + 64))
+            mm(ub, A("g512"), pc(fl), False, True)
+            tt(pc(aout), ub, pc("x1"), OP.min)
+            if last:
+                ts(own(kout, u0, u1), pc(aout), -OFF, OP.add, 0.0, OP.max)
             else:
-                act(pc("sf", k), sbank(k), AF.Identity, bias=0.0 if k < NS else -8 * DOWN, scale=8.0)
-            mm(w, A("g512"), pc("sf", k), False, True)
-            mm(u, A("s32"), pc("sf", k), k < NS, True)
-            if k < NS:
-                act(pc("sr", k), sbank(k), AF.Identity, bias=DOWN)
-
-        def ur(k):
-            act(pc("ur", k), bank(3, k), AF.Identity, bias=DOWN)
-            mm(A("ps7", 0, 128), A("ih"), pc("sr", k), True, False)
-            mm(A("ps7", 0, 128), A("nih"), pc("ur", k), False, True)
-
-        def r1(k):
-            act(pc("r1", k), A("ps7", 0, 128), AF.Relu)
-            u = bank(3, k)
-            mm(u, A("oneb", p1=1), A("kc", 0, 128, p1=1), True, False)
-            mm(u, A("ih"), pc("sr", k), False, False)
-            mm(u, A("nih"), pc("r1", k), False, True)
-
-        def low(k):
-            tt(own(kout, 2 * k, 2 * k + 2), bank(3, k), own(kin, 2 * k, 2 * k + 2), OP.min)
-
-        def x1(k):
-            tt(pc("x1", k), sbank(k), pc("a16", k), OP.min)
-
-        def scn(k):
-            scan(pc("scn", k), A("r64", 0, 128), bank(5, k), OP.min)
-
-        def x2(k):
-            tt(pc("x2", k), bank(3, k), pc("x1", k), OP.min)
-
-        def fin(k, on_v=False):
-            if on_v:
-                ts(own(kout, 2 * k, 2 * k + 2), pc("x2", k), -OFF, OP.add)
-            else:
-                act(own(kout, 2 * k, 2 * k + 2), pc("x2", k), AF.Identity, bias=-OFF)
-
-        def cvt(gi):
-            src = A("scn", 64 * GR[gi][0] + 63, 64 * GR[gi][1], 64)
-            if pas == 0:
-                cp(gc_("mi", gi, 1), src)
-            else:
-                tt(gc_("mi", gi, 1), src, gc_("f%d" % t, gi, 1), OP.min)
-
-        def band(gi):
-            ts(gc_("si%d" % t, gi, 1), gc_("mi", gi, 1), 511, OP.bitwise_and)
-
-        def u16(gi):
-            cp(gc_("su%d" % t, gi, 1), gc_("si%d" % t, gi, 1))
-
-        def out(gi):
-            cp(IND(own(kout, *GR[gi]), gc_("su%d" % t, gi, 1)), A("zero", 0, gn(gi, 16)))
-            send_group(kout, gi)
-
-        def sv(x0, x1_):
-            sg(x0, x1_); vg(x0, x1_)
-
-        sv(0, 16); sv(16, 32); sv(32, 64); ssum(0)
-        sv(64, 96); sg(96, 128); copy(0); vg(96, 128); ssum(1)
-        sg(128, 160); ur(0); vg(128, 160); scn(0); sg(160, 192); r1(0); copy(1); vg(160, 192); ssum(2)
-        sg(192, 224); ur(1); vg(192, 224); scn(1); low(0); sg(224, 256); r1(1); copy(2); vg(224, 256); ssum(3)
-        sg(256, 288); x1(2); scn(2); low(1); x2(2); vg(256, 288); copy(3); fin(2); sg(288, 320)
-        x1(3); scn(3); x2(3); cvt(0); fin(3, True); band(0); sg(320, 352)
-        vg(288, 304); u16(0); vg(304, 320); ssum(4); out(0); sg(352, 368); sg(368, 384)
-        vg(320, 352); copy(4); x1(4); vg(352, 368); scn(4); x2(4); fin(4); vg(368, 384); ssum(5)
-        copy(5); x1(5); scn(5); x2(5); cvt(1); fin(5, True); band(1); u16(1); out(1)
+                act(own(kout, u0, u1), pc(aout), AF.Relu, bias=-OFF)
+            send_done(kout, u1, SR)
+        now.update(side=kout)
+        ts(A("mi"), A("scn", 63, NV, 64), -4.0, OP.mult)
+        ts(A("j%d" % t), A("mi"), 3, OP.bitwise_and)
+        tt(A("si%d" % t), A("j%d" % t), A("base"), OP.add)
+        cp(A("su%d" % t), A("si%d" % t))
 
     def prep_level(pas, t):
-        for gi in range(2):
-            su = gc_("su%d" % t, gi, 1)
-            cp(gc_("e%d" % t, gi, 16), IND(gc_("tri32", gi, 64), su))
-            act(gc_("c%d" % t, gi, 16), IND(gc_("phib", gi, 64), su))
+        for gi in GI:
+            su = G("su%d" % t, gi, 1)
+            cp(G("e%d" % t, gi, 16), IND(G("tri32", gi, 64), su))
+            if t == 0:
+                ts(G("qa", gi, 16), IND(G("tq32", gi, 64), su), float(NW), OP.add)
+            act(G("c%d" % t, gi, 16), IND(G("phib", gi, 64), su))
             if pas == 0:
-                act(gc_("ag%d" % t, gi, 16), IND(own(0, *GR[gi]), su))
-            else:
-                act(gc_("cf%d" % t, gi, 16), IND(gc_("phib", gi, 64), su))
+                if t == 0:
+                    act(G("ag0", gi, 16), IND(own(0, *GR[gi]), su))
+                act(G("jv%d" % t, gi, 16), IND(A("jc"), su))
+        if t == 0:
+            cp(A("kf"), A("e0"))
         if pas == 1:
-            scatter_const(lambda gi: gc_("lev", gi, 64), t, "l%d" % t)
+            act(A("cf%d" % t), A("c%d" % t))
+            if t < 2:
+                act(A("cq%d" % t), A("c%d" % t), AF.Identity, bias=1536.0)
 
-    def lists2(pas):
-        ts(A("j0"), A("si0"), 3, OP.bitwise_and)
-        ts(A("j1"), A("si1"), 3, OP.bitwise_and)
-        ts(A("b4"), A("si0"), 508, OP.bitwise_and)
+    def lists2(pas, kout):
         tt(A("w0"), A("j0"), A("j1"), OP.mult)
         tt(A("w1"), A("j0"), A("j1"), OP.add)
         ts(A("w0"), A("w0"), 0.0, OP.is_equal)
         ts(A("w2"), A("w1"), 1.0, OP.is_equal)
         ts(A("w1"), A("w1"), -1.0, OP.mult, 6.0, OP.add)
         tt(A("w0"), A("w0"), A("w2"), OP.add)
-        tt(A("w1"), A("w1"), A("b4"), OP.add)
-        tt(A("lo"), A("w0"), A("b4"), OP.add)
+        tt(A("w1"), A("w1"), A("base"), OP.add)
+        tt(A("lo"), A("w0"), A("base"), OP.add)
         tt(A("hi"), A("w1"), A("w0"), OP.subtract)
         cp(A("lou"), A("lo"))
         cp(A("hiu"), A("hi"))
-        for src, dst in (("lou", "glo"), ("hiu", "ghi")):
-            for gi in range(2):
-                ts(gc_(dst, gi, 16), IND(gc_("tri32", gi, 64), gc_(src, gi, 1)), -1536.0, OP.add)
-        for bank, l0, l1 in (("ps0", "de", "do"), ("ps7", "se", "so")):
-            mm(A(bank, 0, 192), A(l0), A("glo"), True, False)
-            mm(A(bank, 0, 192), A(l1), A("ghi"), False, True)
-        if pas == 1:
-            tt(A("lop"), A("lo"), A("fx"), OP.max)
-            tt(A("hip"), A("hi"), A("fm"), OP.min)
-        ts(A("lx"), A("ps0", 0, 192), 1536.0, OP.add)
-        ts(A("ly"), A("ps7", 0, 192), 1536.0, OP.add)
+        for src, dst, co in (("lou", "glo", "cl"), ("hiu", "ghi", "ch")):
+            for gi in GI:
+                ts(G(dst, gi, 16), IND(G("tri32", gi, 64), G(src, gi, 1)), -1536.0, OP.add)
+                if pas == 1:
+                    act(G(co, gi, 16), IND(G("ck", gi, 64), G(src, gi, 1)))
+        for s, dst in enumerate(("lx", "ly")):
+            b = A("ps%d" % (2 + s), 0, 192)
+            mm(b, A("p%d0" % s), A("glo"), True, False)
+            mm(b, A("p%d1" % s), A("ghi"), False, True)
+            ts(A(dst), b, 1536.0, OP.add)
+        for gi in GI:
+            w = 64 * (GR[gi][1] - GR[gi][0])
+            b = A("ps%d" % gi, 0, w)
+            mm(b, ONE1, A("kn", 0, w, p1=1), True, False)
+            mm(b, A("gm"), G("fl0", gi, 64), False, False)
+            mm(b, A("gm2"), G("fl1", gi, 64), False, False)
+            mm(b, A("ib"), G("phib", gi, 64), False, True)
+            act(own(kout, *GR[gi]), b)
+        for gi in GI:
+            w = 64 * (GR[gi][1] - GR[gi][0])
+            if pas == 1:
+                b = A("ps4", 0, w)
+                mm(b, ONE1, A("kv", 0, w, p1=1), True, False)
+                mm(b, A("g3"), G("fl0", gi, 64), False, False)
+                mm(b, A("g2"), G("fl1", gi, 64), False, True)
+                act(G("lev", gi, 64), b)
 
     def round2(pas, kin, kout):
         tab = A("tab%d" % kin)
-        ext = arrived(kin)
-        lo, hi = ("lo", "hi") if pas == 0 else ("lop", "hip")
+        now.update(step=kin, side=None)
+        for u0, u1 in R2:
+            gi = group(u0)
+            cuts = list(range(16 * u0, 16 * u1 + 1, 16))
+            if u0 == 0:
+                cuts.insert(1, 8)
+            pair_gathers(tab, kin, "lx", "ly", cuts)
+            n, c = 16 * (u1 - u0), 16 * (u0 - GR[gi][0])
+            o = A("ps%d" % (5 + gi), c, c + n)
+            mm(o, B16, A("bd", 0, n, p1=16), True, False)
+            if pas == 1:
+                mm(o, A("i1k"), U("cl", u0, u1, 16), False, False)
+                mm(o, A("ni1k"), U("ch", u0, u1, 16), False, False)
+            for r in range(16):
+                mm(o, A("gp" if r < 8 else "gn"), A("mn", 256 * u0 + r, 256 * u1, 16), False, r == 15)
+            for gi in ends(u1):
+                n = 16 * (GR[gi][1] - GR[gi][0])
+                scan(G("sc2", gi, 16), A("r16s", 0, n), A("ps%d" % (5 + gi), 0, n), OP.max)
+                tt(G("y2", gi, 1), A("sc2", 16 * GR[gi][0] + 15, 16 * GR[gi][1], 16), G("lo", gi, 1), OP.max)
+                tt(G("si2", gi, 1), G("y2", gi, 1), G("hi", gi, 1), OP.min)
+                cp(G("su2", gi, 1), G("si2", gi, 1))
+                cp(IND(own(kout, *GR[gi]), G("su2", gi, 1)), A("mark", 0, n))
+                send_done(kout, u1, S2)
+        now.update(side=kout)
 
-        def sg(x0, x1):
-            act(A("ga", 16 * x0, 16 * x1), IND(tab, A("lx", x0, x1)), ext=ext)
-
-        def vg(x0, x1):
-            tt(A("mn", 16 * x0, 16 * x1), IND(tab, A("ly", x0, x1)), A("ga", 16 * x0, 16 * x1), OP.min, ext=ext)
-
-        def dsum(k):
-            gi = k // 2
-            o = A("ps%d" % (5 + gi), 64 * (k % 2), 64 * (k % 2) + 64)
-            mm(o, A("b1", p1=16), A("bd", 64 * k, 64 * k + 64, p1=16), True, False)
-            for e in range(2):
-                for m in range(8):
-                    mm(o, A("gp" if e == 0 else "gn"), A("mn", 1024 * k + 2 * m + e, 1024 * k + 1024, 16),
-                       False, e == 1 and m == 7)
-
-        def steps(gi):
-            n = gn(gi, 16)
-            y = gc_("y2", gi, 1)
-
-            def last():
-                cp(IND(own(kout, *GR[gi]), gc_("su2", gi, 1)), A("mark", 0, n))
-                send_group(kout, gi)
-            return [
-                lambda: scan(gc_("sc2", gi, 16), A("r16s", 0, n), A("ps%d" % (5 + gi), 0, n), OP.max),
-                lambda: tt(y, A("sc2", 16 * GR[gi][0] + 15, 16 * GR[gi][1], 16), gc_(lo, gi, 1), OP.max),
-                lambda: tt(gc_("si2", gi, 1), y, gc_(hi, gi, 1), OP.min),
-                lambda: cp(gc_("su2", gi, 1), gc_("si2", gi, 1)),
-                last]
-
-        sg(0, 16)
-        scatter_const(lambda gi: own(kout, *GR[gi]), 1, "mark")
-        vg(0, 16); sg(16, 32); vg(16, 32); sg(32, 48); vg(32, 48); sg(48, 64); vg(48, 64); dsum(0)
-        for x in range(64, 128, 16):
-            sg(x, x + 16); vg(x, x + 16)
-        dsum(1)
-        s0 = steps(0)
-        for i, x in enumerate(range(128, 192, 16)):
-            sg(x, x + 16); vg(x, x + 16)
-            if i == 3:
-                dsum(2)
-            s0[i]()
-        s0[4]()
-        for f in steps(1):
-            f()
-
-    def einit(t):
-        for k in range(3):
-            b = "ps%d" % k
-            mm(A(b), ONE33, K33("ke", 512), True, False)
-            for m in range(8):
-                mm(A(b, 64 * m, 64 * m + 64), A("nib"), A("c%d" % t, 64 * k, 64 * k + 64), False, False)
+    def places(kc):
+        for u in range(0, 12, 2):
+            (act if TG[u // 2] == "a" else cp)(U("mn", u, u + 2, 256), IND(A("tab%d" % kc), U("e0", u, u + 2, 16)), ext=kc)
+        now.update(side=kc + 2)
+        b = A("ps4", 0, 192)
+        mm(b, ONE1, A("kq", p1=1), True, False)
+        for r in range(16):
+            mm(b, A("dm", 128 * r, 128 * r + 128), A("mn", r, NW, 16), False, r == 15)
+        tt(A("tt"), b, A("qa"), OP.min)
+        tt(A("qa"), A("tt"), A("kf"), OP.max)
+        cp(A("f0"), A("qa"))
 
     def level(pas, t, kin, kout):
-        tab = A("tab%d" % kin)
-        ext = arrived(kin)
+        tab = A("tab%d" % kin, 0, NW) if t else A("tab%d" % (kin - 1))
         need_p = not (pas == 0 and t == 0)
-        lst = "e%d" % t
+        lst, c = "e%d" % t if t else "f0", "c%d" % t
+        now.update(step=kin, side=kin)
+        for u0, u1, halves in LP:
+            n = 16 * (u1 - u0)
+            for b, m0, m1 in halves:
+                mm(A("ps%d" % b, 0, n * (m1 - m0)), ONE1, A("ke", 0, n * (m1 - m0), p1=1), True, False)
+                for m in range(m1 - m0):
+                    mm(A("ps%d" % b, n * m, n * m + n), A("nib"), U(c, u0, u1, 16), False, False)
+        now.update(side=None)
+        def part(name, i, m0, m1):
+            u0, u1, _ = LP[i]
+            return A(name, 128 * u0 + 16 * (u1 - u0) * m0, 128 * u0 + 16 * (u1 - u0) * m1)
 
-        def sg(x0, x1):
-            act(A("ga", 16 * x0, 16 * x1), IND(tab, A(lst, x0, x1)), ext=ext)
+        def ebank(i, h):
+            b, m0, m1 = LP[i][2][h]
+            return A("ps%d" % b, 0, 16 * (LP[i][1] - LP[i][0]) * (m1 - m0))
 
-        def vg(x0, x1):
-            cp(A("ga", 16 * x0, 16 * x1), IND(tab, A(lst, x0, x1)), ext=ext)
+        def fetch(i, h):
+            u0, u1, halves = LP[i]
+            n, u = 16 * (u1 - u0), u0
+            while u < u1:
+                v = u + 1
+                while v < min(u1, u + 2) and LG[v] == LG[u]:
+                    v += 1
+                (act if LG[u] == "a" else cp)(U("ga", u, v, 256), IND(tab, U(lst, u, v, 16)), ext=kin)
+                u = v
+            for b, m0, m1 in halves:
+                for r in range(2 * m0, 2 * m1):
+                    x = n * (r // 2 - m0)
+                    mm(A("ps%d" % b, x, x + n), A("ib"), A("ga", 256 * u0 + r, 256 * u1, 16), False, r == 2 * m1 - 1)
 
-        def esum(k):
-            for m in range(8):
-                for s in range(2):
-                    mm(A("ps%d" % k, 64 * m, 64 * m + 64), A("ib"), A("ga", 1024 * k + 2 * m + s, 1024 * k + 1024, 16),
-                       False, m == 7 and s == 1)
+        def z(i, h):
+            act(part("zb", i, *LP[i][2][h][1:]), ebank(i, h), AF.Identity, bias=0.5)
 
-        def part(n, k, m=None):
-            return A(n, 512 * k, 512 * k + 512) if m is None else A(n, 512 * k + 64 * m, 512 * k + 64 * m + 64)
+        def dif(i, h):
+            ms_ = LP[i][2][h][1:]
+            tt(part("db", i, *ms_), ebank(i, h), part("zb", i, *ms_), OP.subtract)
 
-        def z(k):
-            act(part("zb", k), A("ps%d" % k), AF.Identity, bias=0.5)
-
-        def dif(k):
-            tt(part("db", k), A("ps%d" % k), part("zb", k), OP.subtract)
-            if need_p:
-                o = A("ps%d" % (3 + k // 2), 64 * (k % 2), 64 * (k % 2) + 64)
-                mm(o, ONE33, K33("kl", 64), True, False)
-                mm(o, A("ib"), A("c%d" % t, 64 * k, 64 * k + 64), False, False)
-                for m in range(8):
-                    mm(o, A("lu"), part("db", k, m), False, m == 7)
-
-        def thn(k):
-            ts(part("tb", k), part("zb", k), float(2 ** 20), OP.is_lt, A("thf"), OP.mult)
-
-        def absd(k):
-            act(part("ab", k), part("db", k), AF.Abs)
-            o = A("ps%d" % (5 + k // 2), 64 * (k % 2), 64 * (k % 2) + 64)
-            for m in range(8):
-                mm(o, A("gn"), part("tb", k, m), m == 0, False)
-            for m in range(8):
-                mm(o, A("gp"), part("ab", k, m), False, m == 7)
-
-        def zz(gi):
-            if need_p:
-                act(gc_("zz", gi, 16), A("ps%d" % (3 + gi), 0, gn(gi, 16)), AF.Identity, bias=-1663.5)
-
-        def phase(gi):
-            if need_p:
-                tt(gc_("rr", gi, 16), A("ps%d" % (3 + gi), 0, gn(gi, 16)), gc_("zz", gi, 16), OP.subtract)
-                ts(gc_("pb", gi, 16), gc_("rr", gi, 16), -1536.0, OP.add)
-
-        def post(gi):
-            if t > 0:
-                ts(gc_("mk", gi, 16), A("ps%d" % (5 + gi), 0, gn(gi, 16)), 0.0, OP.is_gt, MARK, OP.mult)
-                tt(IND(own(kout, *GR[gi]), gc_("su%d" % t, gi, 1)), gc_("pb", gi, 16), gc_("mk", gi, 16), OP.add)
+        def size(i, h):
+            ms_ = LP[i][2][h][1:]
+            if i in ABS:
+                act(part("ab", i, *ms_), part("db", i, *ms_), AF.Abs)
             else:
-                record(gi)
-            if t > 0 or pas == 0:
-                send_group(kout, gi)
-            else:
-                c0, c1 = 64 * GR[gi][0], 64 * GR[gi][1]
-                store(T.yphi[:, c0:c1], A("pout", c0, c1), "d_y%d" % gi)
+                ts(part("ab", i, *ms_), part("db", i, *ms_), 0.0, OP.max)
 
-        def record(gi):
-            su = gc_("su%d" % t, gi, 1)
-            if pas == 1:
-                tt(gc_("dd", gi, 16), gc_("pb", gi, 16), gc_("c%d" % t, gi, 16), OP.subtract)
-            ts(gc_("nk", gi, 16), A("ps%d" % (5 + gi), 0, gn(gi, 16)), 0.0, OP.is_le)
-            if pas == 0:
-                tt(IND(own(6, *GR[gi]), su), gc_("ag%d" % t, gi, 16), gc_("nk", gi, 16), OP.mult)
+        def limit(i, h):
+            ms_ = LP[i][2][h][1:]
+            if i in THS:
+                act(part("tb", i, *ms_), part("zb", i, *ms_), AF.Relu, bias=A("thf"), scale=-2.0 ** -30)
             else:
-                tt(gc_("tt", gi, 16), gc_("dd", gi, 16), gc_("nk", gi, 16), OP.mult)
-                tt(IND(gc_("pout", gi, 64), su), gc_("tt", gi, 16), gc_("cf%d" % t, gi, 16), OP.add)
+                ts(part("tb", i, *ms_), part("zb", i, *ms_), float(2 ** 20), OP.is_lt, A("thf"), OP.mult)
 
-        sg(0, 32); vg(32, 64); esum(0)
-        sg(64, 96); vg(96, 128); esum(1)
-        z(0); vg(160, 192); sg(128, 160); dif(0); thn(0); esum(2)
-        z(1); absd(0); dif(1); thn(1)
-        z(2); absd(1); zz(0); dif(2); thn(2); absd(2)
-        phase(0); post(0); zz(1); phase(1); post(1)
+        def sums(i, h):
+            u0, u1, halves = LP[i]
+            gi = group(u0)
+            n, o = 16 * (u1 - u0), 16 * (u0 - GR[gi][0])
+            _, m0, m1 = halves[h]
+            tb, xb = A("ps%d" % (3 + gi), o, o + n), A("ps%d" % (5 + gi), o, o + n)
+            terms = (("xn", "tb"), ("xp", "ab")) if i in ABS else (("xn", "tb"), ("xn", "db"), ("xp2", "ab"))
+            if need_p:
+                if h == 0:
+                    mm(tb, ONE33, A("kl", 0, n, p1=33), True, False)
+                    mm(tb, A("ib"), U(c, u0, u1, 16), False, False)
+                for m in range(m0, m1):
+                    mm(tb, A("lu"), part("db", i, m, m + 1), False, m == 7)
+            if t == 1 and h == 0:
+                mm(xb, ONE1, A("kx", 0, n, p1=1), True, False)
+            for j, (l, r) in enumerate(terms):
+                for m in range(m0, m1):
+                    mm(xb, A(l), part(r, i, m, m + 1), t != 1 and j == 0 and m == 0, j == len(terms) - 1 and m == 7)
+            if m1 == 8:
+                for gi in ends(u1):
+                    finish(pas, t, kout, gi)
+
+        call = {"f": fetch, "z": z, "d": dif, "a": size, "l": limit, "s": sums}
+        for w in LO.split():
+            call[w[0]](int(w[1]), int(w[2:] or 0))
+
+    def finish(pas, t, kout, gi):
+        n = 16 * (GR[gi][1] - GR[gi][0])
+        tb, xb = A("ps%d" % (3 + gi), 0, n), A("ps%d" % (5 + gi), 0, n)
+        su = G("su%d" % t, gi, 1)
+
+        def h(name):
+            return G(name, gi, 16)
+        if pas == 1 or t > 0:
+            act(h("zz"), tb, AF.Identity, bias=-1663.5)
+            tt(h("rr"), tb, h("zz"), OP.subtract)
+        if t == 2:
+            ts(h("pb"), h("rr"), -1536.0, OP.add)
+            ts(h("mk"), xb, 0.0, OP.is_gt, MARK, OP.mult)
+            tt(IND(own(kout, *GR[gi]), su), h("pb"), h("mk"), OP.add)
+            send_done(kout, GR[gi][1], SL)
+        if t == 1:
+            o = NW + 192 * rank
+            ts(h("pb"), xb, MARK, OP.min, -1536.0, OP.max)
+            tt(A("tab%d" % (kout - 1), o + 16 * GR[gi][0], o + 16 * GR[gi][1]), h("rr"), h("pb"), OP.add)
+            if GR[gi][1] == 12:
+                send(kout, A("tab%d" % (kout - 1), o, o + 192))
         if t > 0:
-            if t == 2:
-                act(own(kout + 1), own(kout))
-            record(0); record(1)
+            now.update(side=kout)
+        if pas == 1 or t == 0:
+            ts(h("nk"), xb, 0.0, OP.is_le)
         if pas == 0:
-            mm(A("ps7", 0, 192), A("b1", p1=16), A("bd", p1=16), True, False)
-            mm(A("ps7", 0, 192), A("ib"), A("nk"), False, True)
-            scan(A("sc2"), A("r16s"), A("ps7", 0, 192), OP.max)
-            ts(A("w3"), A("sc2", 15, 192, 16), float(2 ** 26), OP.mult, -512.0, OP.add)
-            tt(A("k%d" % t), A("w3"), A("si%d" % t), OP.add)
-
-    def forced():
-        tt(A("w0"), A("k0"), A("k1"), OP.min)
-        tt(A("w1"), A("k0"), A("k1"), OP.max)
-        tt(A("f0"), A("w0"), A("k2"), OP.min)
-        tt(A("w2"), A("w1"), A("k2"), OP.min)
-        tt(A("w1"), A("w1"), A("k2"), OP.max)
-        tt(A("f1"), A("w0"), A("w2"), OP.max)
-        ts(A("fm"), A("w1"), 512.0, OP.add)
-        ts(A("w3"), A("w1"), 1000.0, OP.is_gt, -float(2 ** 27), OP.mult)
-        tt(A("fx"), A("fm"), A("w3"), OP.add)
+            if t == 0:
+                tt(IND(own(6, *GR[gi]), su), h("ag0"), h("nk"), OP.mult)
+                send_done(kout, GR[gi][1], SL)
+                now.update(side=kout)
+            if t < 2:
+                ts(h("mk"), xb, 0.0, OP.is_gt, MARK, OP.mult)
+            tt(IND(G("ck", gi, 64), su), h("jv%d" % t), h("mk"), OP.mult)
+        else:
+            if t == 2:
+                tt(h("dd"), h("pb"), h("c%d" % t), OP.subtract)
+            else:
+                tt(h("dd"), h("rr"), h("cq%d" % t), OP.subtract)
+            tt(h("tt"), h("dd"), h("nk"), OP.mult)
+            tt(IND(G("pout", gi, 64), su), h("tt"), h("cf%d" % t), OP.add)
+            if t == 0:
+                store(T.yphi[:, 64 * GR[gi][0]:64 * GR[gi][1]], G("pout", gi, 64), "d_y%d" % gi)
+        now.update(side=None)
 
     for pas in range(2):
         k = 6 * pas
-        if pas == 1:
-            forced()
-            prep_a16(k)
         round01(pas, 0, k, k + 1)
-        prep_a16(k + 1)
-        act(own(k + 3), A("phib"))
-        scatter_const(lambda gi: gc_("dp%d" % pas, gi, 64), 0, "big")
         prep_level(pas, 0)
-        scatter_const(lambda gi: own(k + 3, *GR[gi]), 0, "mark")
         round01(pas, 1, k + 1, k + 2)
-        lists2(pas)
+        lists2(pas, k + 3)
+        prep_level(pas, 1)
         round2(pas, k + 2, k + 3)
         prep_level(pas, 2)
-        einit(2)
-        act(own(k + 4), own(k + 3))
-        prep_level(pas, 1)
-        if pas == 0:
-            act(own(6), own(0))
-        else:
-            rec("s", lambda: g.sync.dma_start(T.ylev[:], T.lev[0:128:16, :]), [], [A("lev")], sem="d_lev")
+        for gi in GI:
+            act(own(k + 4, *GR[gi]), own(k + 3, *GR[gi]))
+        if pas == 1:
+            for gi in GI:
+                cp(IND(G("lev", gi, 64), G("su2", gi, 1)), A("l2", 0, 16 * (GR[gi][1] - GR[gi][0])))
+            rec("s", lambda: g.sync.dma_start(T.ylev[:], T.lev[0:128:16, :]), [], [A("lev")], 0.1, sem="d_lev", lag=LAT)
         level(pas, 2, k + 3, k + 4)
-        einit(1)
-        if pas == 0:
-            ms(A("dp1"), 0.0)
-            ms(A("lev"), 3.0)
-            for i in range(3):
-                ms(A("l%d" % i), float(i))
+        now.update(side=k + 4)
+        places(k + 3)
         level(pas, 1, k + 4, k + 5)
-        einit(0)
         if pas == 0:
-            act(A("pout"), A("phib"))
+            now.update(side=5)
+            for gi in GI:
+                b = A("ps%d" % (3 + gi), 0, 64 * (GR[gi][1] - GR[gi][0]))
+                mm(b, A("ib"), own(0, *GR[gi]), True, False)
+                mm(b, A("ib"), G("ck", gi, 64), False, True)
+                act(own(6, *GR[gi]), b, AF.Relu)
         level(pas, 0, k + 5, k + 6)
 
-    hist, seq = {}, {}
-    known = {q: {} for q in "vapgs"}
+    emit(g, T, ops, sends, per_send)
+
+
+def emit(g, T, ops, sends, per_send):
+    hist, bank = {}, {}
     for i, o in enumerate(ops):
-        q = o["q"]
-        deps = set()
+        deps, after = set(), {}
         touched = [(d, False) for d in o["rd"]] + [(d, True) for d in o["wr"]]
         for d, w in touched:
-            h = hist.setdefault(d[0], [])
             if d[0].startswith("ps"):
-                for (lo_, hi_, j, jw) in h:
-                    if ops[j]["q"] != q or (q != "p" and (w or jw)):
+                j = bank.get(d[0])
+                if j is not None and j != i:
+                    if ops[j]["q"] == o["q"]:
+                        after[j] = 0.0
+                    else:
                         deps.add(j)
+                bank[d[0]] = i
             else:
-                for (lo_, hi_, j, jw) in h:
-                    if (w or jw) and lo_ < d[2] and d[1] < hi_:
+                for (lo, hi, j, jw) in hist.setdefault(d[0], []):
+                    if (w or jw) and lo < d[2] and d[1] < hi and j != i:
                         deps.add(j)
-        deps.discard(i)
         for d, w in touched:
-            h = hist[d[0]]
-            if d[0].startswith("ps"):
-                h[:] = [e for e in h if ops[e[2]]["q"] != q or (e[3] and not w)]
-            elif w and d[3] == 1 and d[4] == 0 and d[5] == 128:
-                h[:] = [e for e in h if not (d[1] <= e[0] and e[1] <= d[2])]
-            elif not w:
-                h[:] = [e for e in h if e[3] or ops[e[2]]["q"] != q or ops[e[2]]["sem"]
-                        or not (d[1] <= e[0] and e[1] <= d[2])]
-            h.append((d[1], d[2], i, w))
-        kn = known[q]
+            if not d[0].startswith("ps"):
+                h = hist[d[0]]
+                if w and d[3] == 1 and d[4] == 0 and d[5] == 128:
+                    h[:] = [e for e in h if not (d[1] <= e[0] and e[1] <= d[2])]
+                h.append((d[1], d[2], i, w))
+        for j in deps:
+            after[j] = HOP if ops[j]["sem"] == "none" else ops[j]["lag"]
+        if o["ext"] is not None:
+            js = sends[o["ext"]]
+            for n, j in enumerate(js):
+                after[j] = LAT + sum(ops[x]["lag"] for x in js[n:])
+        o["deps"], o["after"], o["succ"] = deps, after, []
+    allsends = sorted(j for js in sends.values() for j in js)
+    for a, b in zip(allsends[:-1], allsends[1:]):
+        ops[b]["after"].setdefault(a, 0.0)
+    for i, o in enumerate(ops):
+        for j in o["after"]:
+            ops[j]["succ"].append(i)
+    for o in reversed(ops):
+        o["due"] = o["step"] if o["side"] is None else min([99] + [ops[s]["due"] for s in o["succ"]])
+    for i in range(len(ops) - 1, -1, -1):
+        o = ops[i]
+        o["rank"] = i if o["side"] is None else min([len(ops)] + [ops[s]["rank"] for s in o["succ"]])
+    closing = {js[-1]: k for k, js in sends.items() if k < 12}
+    owed, todo = {}, {}
+    opening = {}
+    for i, o in enumerate(ops):
+        if o["side"] is None:
+            opening.setdefault(o["step"], i)
+    for o in ops:
+        if o["side"] is not None:
+            o["urgent"] = o["rank"] < opening.get(o["due"], 0) + 8
+            owed[o["q"], o["due"]] = owed.get((o["q"], o["due"]), 0) + o["urgent"]
+        else:
+            todo[o["q"], o["step"]] = todo.get((o["q"], o["step"]), 0) + 1
+    sent, end = -1, LAT + 0.5
+    free = {q: 0.0 for q in "vapgs"}
+    done = {q: 0.0 for q in "vapgs"}
+    left = [len(o["after"]) for o in ops]
+    ready = {i: 0.0 for i, n in enumerate(left) if n == 0}
+    order = []
+    while ready:
+        best = None
+        for q in free:
+            main = [j for j in ready if ops[j]["q"] == q and ops[j]["side"] is None]
+            t = max(free[q], min([ready[j] for j in main], default=1e9))
+            pick = min([j for j in main if ready[j] <= t + HOP], default=None)
+            at = 1e9 if pick is None else max(free[q], ready[pick])
+            pause, limit = sent, end
+            if sent >= 0 and not todo.get((q, sent)):
+                pause, limit = sent + 1, done[q] + EARLY + ROOM
+            fill = []
+            for j in ready:
+                o = ops[j]
+                if o["q"] == q and o["side"] is not None and min(o["side"], o["due"]) <= pause:
+                    s = max(free[q], ready[j])
+                    fits = s + o["cost"] <= min(at, limit) + HOP
+                    if o["due"] <= pause:
+                        ok = s <= at and (fits or pick is None or o["rank"] < pick)
+                    else:
+                        ok = fits and not owed.get((q, pause))
+                    if ok or pause == 12:
+                        fill.append((round(s, 1), o["rank"], j))
+            if fill and min(fill)[0] <= at:
+                at, _, pick = min(fill)
+            if pick is not None and (best is None or at < best[0]):
+                best = (at, pick)
+        i = best[1]
+        q = ops[i]["q"]
+        start = max(ready.pop(i), free[q])
+        ops[i]["end"] = free[q] = start + ops[i]["cost"]
+        if ops[i]["side"] is not None:
+            owed[q, ops[i]["due"]] -= ops[i]["urgent"]
+        else:
+            todo[q, ops[i]["step"]] -= 1
+            done[q] = free[q]
+        if i in closing:
+            sent, end = closing[i], start + ROOM * (1 if closing[i] else 2)
+        order.append(i)
+        for s in ops[i]["succ"]:
+            left[s] -= 1
+            if left[s] == 0:
+                ready[s] = max(ops[j]["end"] + lag for j, lag in ops[s]["after"].items())
+    seq, place = {}, {}
+    known = {q: {} for q in "vapgs"}
+    for n, i in enumerate(order):
+        o = ops[i]
+        place[i] = n
+        kn = known[o["q"]]
         waits = []
-        if o["ext"] and kn.get(o["ext"][0], 0) < o["ext"][1]:
-            waits.append(o["ext"])
-            kn[o["ext"][0]] = o["ext"][1]
-        for j in sorted(deps, reverse=True):
+        if o["ext"] is not None:
+            s, v = "arr%d" % o["ext"], per_send * len(sends[o["ext"]])
+            if kn.get(s, 0) < v:
+                waits.append((s, v))
+                kn[s] = v
+        for j in sorted(o["deps"], key=lambda j: -place[j]):
+            if ops[j]["sem"] == "none":
+                raise ValueError("a table that is being sent is written again")
             key, val = ops[j]["done"]
             if kn.get(key, 0) >= val:
                 continue
@@ -643,12 +730,13 @@ def rank_program(g, core, T, topo):
             kn[key] = val
         o["waits"] = waits
         o["clock"] = dict(kn)
-        key = o["sem"] or q
+        key = o["sem"] or o["q"]
         seq[key] = seq.get(key, 0) + (16 if o["sem"] else 1)
         o["done"] = (key, seq[key])
     eng = {"v": g.vector, "a": g.scalar, "p": g.tensor, "g": g, "s": g.sync}
     cnt = {}
-    for o in ops:
+    for i in order:
+        o = ops[i]
         q = o["q"]
         for w in o["waits"]:
             s, v = w if isinstance(w, tuple) else ops[w]["sig"]
@@ -663,6 +751,6 @@ def rank_program(g, core, T, topo):
             cnt[QSEM[q]] = cnt.get(QSEM[q], 0) + 1
             ins.then_inc(T.sem[QSEM[q]], 1)
             o["sig"] = (QSEM[q], cnt[QSEM[q]])
-    g.wait_ge(T.sem.sent, nsent[0])
+    g.wait_ge(T.sem.sent, per_send * len(allsends))
     for s in ("d_lev", "d_y0", "d_y1"):
         g.sync.wait_ge(T.sem[s], 16)

@@ -1,25 +1,44 @@
 from concourse.bass import DstId, RemoteDMATransfer
-from concourse.mybir import AluOpType, ActivationFunctionType
+from concourse.mybir import AluOpType, ActivationFunctionType, AxisListType
 
 NV, NW = 768, 3072
 GR = [(0, 8), (8, 12)]
 FIRST = [(0, 6), (6, 12)]
 SR = [(0, 4), (4, 8), (8, 12)]
+GAP = "t1"
+T6V = ()
+R1 = 0
+CKG = (0,)
+CKW = 0
+WAY = 2.0
+C1 = [0, 16, 48, 64, 96, 128, 160, 192, 224, 256, 288, 320, 352, 372, 384]
+SOLO = 16
+AHEAD = 0
+LATE = 0
+CAP6 = 60
+C2 = [0, 16, 48, 64, 96, 128, 144, 160, 176, 192]
 EARLY = 0.5
-ROOM = 3.2
+ONCE = 2.5
+ROOM0 = 2.5
+ROOM = 2.0
 S2 = [(0, 8), (8, 12)]
 SL = [(0, 12)]
 RP = [(0, 2), (2, 4), (4, 6), (6, 8), (8, 10), (10, 11), (11, 12)]
-R2 = [(0, 4), (4, 8), (8, 11), (11, 12)]
+R2 = [(0, 4), (4, 8), (8, 12)]
 LP = [(0, 4, [(0, 0, 8)]), (4, 8, [(1, 0, 8)]), (8, 12, [(2, 0, 4), (7, 4, 8)])]
-LG = "aavvaavvavvv"
-LO = "f0 f1 z0 f2 z1 d0 z20 d1 z21 a0 l0 d20 a1 l1 d21 s0 s1 a20 l20 a21 l21 s20 s21"
-TG = "avaava"
+LG = [[("a", 28), ("v", 36)], [("a", 32), ("v", 32)], [("a", 24), ("v", 40)]]
+THC = (0,)
+LO = "f0 f1 f2 o0 o1 z0 z1 d0 z20 d1 z21 a0 d20 a1 d21 t0 b20 b21 l0 t1 s0 s1 a20 a21 t20 t21 s20 s21"
+TG = {0: "avavaa", 1: "avavaa"}
 NEAR = 4
-THS = ()
-ABS = (0, 1, 2)
+RELU = ()
+ZV = ()
+ZZV = ()
 OFF = 1088.0
 MARK = float(2 ** 42)
+MARK2 = float(2 ** 70)
+NEW = {2: 4096, 1: 5120}
+NONE = NEW[2] + NV
 BF, F16, F32, I32, U16 = "bfloat16", "float16", "float32", "int32", "uint16"
 
 SCRATCH = {}
@@ -40,24 +59,27 @@ def _pack(base, dt, cols, names):
 
 _sb(I32, NV, "amp32 phi32 tri32 tq32")
 _sb(I32, 1, "th32")
-_sb(F32, 1, "thf")
-_sb(BF, NW, "tab0 tab1 tab2 tab3 tab6 tab7 tab8 tab9")
-_sb(BF, NW + NV, "tab4 tab10")
+_sb(F32, 8, "thf")
+_sb(BF, 8, "thb")
+_sb(F32, 16, "srow")
+_sb(BF, NW, "tab0 tab1 tab2 tab6 tab7 tab8")
+_sb(BF, NEW[1] + NV, "tab3 tab9")
 _sb(BF, 6144, "ga mn")
 _sb(BF, 1536, "zb db ab tb")
 _sb(U16, 384, "offa offb")
-_pack("l192", U16, 192, "lx ly e0 e1 e2 f0")
+_pack("l192", U16, 192, "lx ly e0 e1 e2 f0 f1")
 _sb(F16, NV, "r16 x1 xa xb sf")
 _sb(F32, NV, "scn pout lev")
 _sb(BF, NV, "phib fl0 fl1 ck")
-_pack("h192", F16, 192, "glo ghi rr")
-_pack("b192", BF, 192, "c0 c1 c2 ag0 jv0 jv1 jv2 cl ch zz pb mk nk dd bd kq")
-_pack("f192", F32, 192, "cf0 cf1 cf2 cq0 cq1 tt r16s sc2 qa kf")
-_sb(F32, 128, "r64 l2")
-_sb(BF, 512, "ke kn kv jc pick")
+_pack("h192", F16, 192, "glo ghi rr0 rr1 rr2 qh0 qh1")
+_pack("b192", BF, 192, "c0 c1 c2 ag0 jv0 jv1 jv2 cl ch zz pb mk0 mk1 mk2 nk0 nk1 nk2 dd bd")
+_pack("f192", F32, 192, "cf0 cq0 tt tq tq1 tq2 r16s sc2 kf0 kf1")
+_sb(F32, 128, "r64")
+_sb(BF, 512, "ke km kn kv jc pick")
 _sb(BF, 2048, "dm")
-_pack("b128", BF, 128, "oneb ib nib i8 i20 i1k ni1k gt gp gn xp xp2 xn g1n g512 g3 g2 gm gm2 b1 lu s64 ks ku kl kb kx mark")
-_pack("h128", F16, 128, "p00 p01 p10 p11 gh s32")
+_pack("b128", BF, 128, "oneb ib nib i8 i20 i1k ni1k gt gp gn xp xp2 xn g1n g512 g3 g2 gm gm1 i70 b1 lu s64 ks ku kl kb kx mark"
+      " th0 th1 tl0 tl1 vf")
+_pack("h128", F16, 128, "p00 p01 p10 p11 gh s32 ih")
 _pack("smi", I32, 12, "mi si0 si1 si2 j0 j1 io0 io1")
 _pack("smu", U16, 12, "su0 su1 su2 lou hiu")
 _pack("smf", F32, 12, "w0 w1 w2 lo hi y2 base")
@@ -69,7 +91,8 @@ SEMAPHORES = (["sv", "sa", "sp", "sg", "sent", "d_a0", "d_a1", "d_tri", "d_phi",
 QSEM = {"v": "sv", "a": "sa", "p": "sp", "g": "sg"}
 OP = AluOpType
 AF = ActivationFunctionType
-CYC, GAT, SCA, PEC, HOP, LAT, ROW, BYTE = 0.0009, 1.56, 3.8, 0.0005, 0.1, 2.5, 0.045, 0.00005
+COSTS = (0.0009, 1.56, 3.8, 0.0005, 0.1, 2.5, 0.045, 0.00005)
+CYC, GAT, SCA, PEC, HOP, LAT, ROW, BYTE = COSTS
 
 
 def A(name, c0=0, c1=None, step=1, p0=0, p1=128):
@@ -124,6 +147,7 @@ def rank_program(g, core, T, topo):
                     rd.append(d[1]); rd.append(d[2])
                 else:
                     rd.append(d)
+        ext = () if ext is None else ext if isinstance(ext, tuple) else (ext,)
         ops.append({"q": q, "fn": fn, "rd": rd, "wr": wr, "ext": ext, "sem": sem, "cost": cost, "lag": lag, **now})
 
     def dur(o, i, per=None):
@@ -155,7 +179,7 @@ def rank_program(g, core, T, topo):
         rec("v", lambda: g.vector.tensor_tensor_scan(ap(o), ap(d0), ap(d1), 0.0, OP.add, op1), [o], [d0, d1], dur(o, d1))
 
     def act(o, i, func=AF.Copy, bias=0.0, scale=1.0, ext=None):
-        rec("a", lambda: g.scalar.activation(ap(o), ap(i), func, bias=ap(bias), scale=scale), [o], [i, bias],
+        rec("a", lambda: g.scalar.activation(ap(o), ap(i), func, bias=ap(bias), scale=ap(scale)), [o], [i, bias, scale],
             dur(o, i, 1.0), ext)
 
     def mm(o, l, r, start, stop):
@@ -185,7 +209,7 @@ def rank_program(g, core, T, topo):
     for i, c in enumerate(far):
         masks[c] = sum(1 << e for e in off_eng[i * share:(i + 1) * share])
     per_send = len(on_eng) + share * len(far)
-    sends = {}
+    sends, later = {}, {}
 
     def own(k, u0=0, u1=12):
         return A("tab%d" % k, rank * NV + 64 * u0, rank * NV + 64 * u1)
@@ -199,7 +223,7 @@ def rank_program(g, core, T, topo):
                                              remote_sem=T.sem["arr%d" % k], src=ap(d), dst=ap(d)))
             g.remote_dma_fused(trs, local_sem=T.sem.sent)
         sends.setdefault(k, []).append(len(ops))
-        rec("g", fn, [], [d], 0.3, sem="none", lag=128 // share * (ROW + 2 * BYTE * width(d)))
+        rec("g", fn, [], [d], 0.3 if k else ONCE, sem="none", lag=128 // share * (ROW + 2 * BYTE * width(d)))
 
     def send_done(k, u1, parts):
         for a, b in parts:
@@ -257,13 +281,12 @@ def rank_program(g, core, T, topo):
         ms(A(n, p1=64), 0.0)
         ms(A(n, p1=1), a)
         ms(A(n, p0=32, p1=33), b)
-    for n, a in (("ke", 49152.0), ("kv", -77.0), ("kn", 48 * MARK), ("kx", -2 * MARK), ("kq", -4096.0)):
+    for n, a in (("ke", 49152.0), ("kv", -57.0), ("kn", 16 * MARK), ("kx", -2 * MARK), ("km", 20 * MARK2)):
         ms(A(n, p1=1), a)
     ms(A("r64"), 0.0)
     ms(A("r64", 0, 128, 64), -float(2 ** 26))
     ms(A("r16s"), 0.0)
     ms(A("r16s", 0, 192, 16), -4 * MARK)
-    ms(A("l2"), 2.0)
     ms(A("ck"), 0.0)
     ts(A("r16"), A("tri32"), -1536.0, OP.add)
     for s, dst in enumerate(("offa", "offb")):
@@ -273,29 +296,48 @@ def rank_program(g, core, T, topo):
     mm(A("ps5", 0, 128), B16, B16, True, True)
     ts(A("s32"), A("ps5", 0, 128), 1.0 / 32, OP.mult)
     ts(A("s64"), A("ps5", 0, 128), 1.0 / 64, OP.mult)
-    for n, f in (("i8", 0.125), ("nib", -1.0), ("i20", 2.0 ** 20), ("i1k", 1024.0), ("ni1k", -1024.0)):
+    ts(A("srow"), A("ps5", 0, 16), 4096 / MARK2, OP.mult)
+    cp(A("ih"), A("ib"))
+    for n, f in (("i8", 0.125), ("nib", -1.0), ("i20", 2.0 ** 20), ("i1k", 1024.0), ("ni1k", -1024.0),
+                 ("i70", -1 / MARK2)):
         ts(A(n), A("ib"), f, OP.mult)
     for n, f in (("gh", -1.0), ("g1n", -1.0), ("g512", 512.0), ("gp", 1024.0), ("gn", -1024.0), ("xp", 4 * MARK),
-                 ("xp2", 8 * MARK), ("xn", -4 * MARK), ("gm", -MARK), ("gm2", -2 * MARK), ("g3", 3.0), ("g2", 2.0)):
+                 ("xp2", 8 * MARK), ("xn", -4 * MARK), ("gm", -MARK), ("gm1", -1.25 * MARK2), ("g3", 3.0), ("g2", 0.75)):
         ts(A(n), A("gt"), f, OP.mult)
     tt(A("lu"), A("s64"), A("i8"), OP.add)
     cp(A("phib"), A("phi32"))
-    cp(A("thf"), A("th32"))
+    cp(A("thb", 0, 1), A("th32"))
+    cp(A("thf", 2, 3), A("th32"))
+    mm(A("ps4", 0, 1), A("gt"), A("thb", 0, 1), True, True)
+    cp(A("thb", 1, 2), A("ps4", 0, 1))
+    tt(A("thb", 2, 3), A("ps4", 0, 1), A("thb", 1, 2), OP.subtract)
+    rec("v", lambda: g.vector.tensor_reduce(ap(A("thf", 0, 1)), ap(A("s64", 0, 8)), AxisListType.X, OP.add),
+        [A("thf", 0, 1)], [A("s64", 0, 8)], 64 * CYC)
+    ts(A("thf", 1, 2), A("thf", 0, 1), -1.0, OP.mult, 1.0 / 64, OP.add)
+    for h in range(2):
+        for c, n in ((1, "th"), (2, "tl")):
+            ts(A("thf", 2 + 2 * h + c, 3 + 2 * h + c), A("thf", h, h + 1), A("thb", c, c + 1), OP.mult, 64.0, OP.mult)
+            ts(A(n + str(h)), A("xn"), A("thf", 2 + 2 * h + c, 3 + 2 * h + c), OP.mult)
     ts(A("tq32"), A("tri32"), 2, OP.arith_shift_right)
     for r in range(16):
-        ts(A("dm", 128 * r, 128 * r + 128), A("ib"), A("s64", r, r + 1), OP.mult, 64 * 4096 / MARK, OP.mult)
-    ms(A("mark"), MARK)
+        act(A("dm", 128 * r, 128 * r + 128), A("ib"), AF.Identity, scale=A("srow", r, r + 1))
+    for k in (3, 9):
+        ms(A("tab%d" % k, NW, NEW[2]), MARK)
+        ms(A("tab%d" % k, NONE, NEW[1]), MARK)
+    ms(A("mark"), MARK2)
     act(A("pout"), A("phib"))
 
     def pair_gathers(tab, k, la, lb, cuts):
         for x0, x1 in zip(cuts[:-1], cuts[1:]):
-            act(A("ga", 16 * x0, 16 * x1), IND(tab, A(la, x0, x1)), ext=k)
+            (act if x0 else cp)(A("ga", 16 * x0, 16 * x1), IND(tab, A(la, x0, x1)), ext=k)
             tt(A("mn", 16 * x0, 16 * x1), IND(tab, A(lb, x0, x1)), A("ga", 16 * x0, 16 * x1), OP.min, ext=k)
 
     def round01(pas, t, kin, kout):
         tab = A("tab%d" % kin)
         ain, aout = ("xb", "xa") if t == 0 else ("xa", "xb")
-        fl = "fl%d" % t
+
+        def fl(u0, u1):
+            return U("fl%d" % t, u0, u1, 64)
         now.update(step=kin, side=kin)
         if t == 0:
             act(A(ain), own(kin), AF.Identity, bias=OFF)
@@ -303,11 +345,7 @@ def rank_program(g, core, T, topo):
         for i, (u0, u1) in enumerate(RP):
             w = 64 * (u1 - u0)
             last = u1 == 12
-            cuts = list(range(32 * u0, 32 * u1 + 1, 32))
-            if u0 == 0:
-                cuts.insert(1, 8)
-            if last:
-                cuts.insert(-1, cuts[-1] - 12)
+            cuts = [x for x in C1 if 32 * u0 <= x <= 32 * u1]
             pair_gathers(tab, kin, "offa", "offb", cuts)
             sb, kb, ub = (A("ps%d" % b, 0, w) for b in (i % 3, 3 + i % 2, 5 + i % 3))
 
@@ -324,6 +362,14 @@ def rank_program(g, core, T, topo):
             if last:
                 for m in range(8):
                     mm(kb, A("g1n"), trip(m), False, m == 7)
+
+            def choose():
+                scan(pc("scn"), A("r64", 0, w), kb, OP.max)
+                for u in range(u0, u1):
+                    act(fl(u, u + 1), A(kb[0], 64 * (u - u0), 64 * (u - u0) + 64), AF.Sign, scale=-1.0,
+                        bias=A("scn", 64 * u + 63, 64 * u + 64))
+            if last:
+                choose()
             mm(sb, ONE33, A("ks", 0, w, p1=33), True, False)
             for m in range(8):
                 mm(sb, A("i8"), trip(m), False, m == 7)
@@ -333,11 +379,9 @@ def rank_program(g, core, T, topo):
                 mm(kb, A("gh"), pc("sf"), False, True)
             mm(ub, ONE33, A("ku", 0, w, p1=33), True, False)
             mm(ub, A("s32"), pc("sf"), False, False)
-            scan(pc("scn"), A("r64", 0, w), kb, OP.max)
-            for u in range(u0, u1):
-                act(U(fl, u, u + 1, 64), A(kb[0], 64 * (u - u0), 64 * (u - u0) + 64), AF.Sign, scale=-1.0,
-                    bias=A("scn", 64 * u + 63, 64 * u + 64))
-            mm(ub, A("g512"), pc(fl), False, True)
+            if not last:
+                choose()
+            mm(ub, A("g512"), fl(u0, u1), False, True)
             tt(pc(aout), ub, pc("x1"), OP.min)
             if last:
                 ts(own(kout, u0, u1), pc(aout), -OFF, OP.add, 0.0, OP.max)
@@ -354,19 +398,18 @@ def rank_program(g, core, T, topo):
         for gi in GI:
             su = G("su%d" % t, gi, 1)
             cp(G("e%d" % t, gi, 16), IND(G("tri32", gi, 64), su))
-            if t == 0:
-                ts(G("qa", gi, 16), IND(G("tq32", gi, 64), su), float(NW), OP.add)
+            if t < 2:
+                cp(G("qh%d" % t, gi, 16), IND(G("tq32", gi, 64), su))
             act(G("c%d" % t, gi, 16), IND(G("phib", gi, 64), su))
             if pas == 0:
                 if t == 0:
                     act(G("ag0", gi, 16), IND(own(0, *GR[gi]), su))
                 act(G("jv%d" % t, gi, 16), IND(A("jc"), su))
-        if t == 0:
-            cp(A("kf"), A("e0"))
-        if pas == 1:
-            act(A("cf%d" % t), A("c%d" % t))
-            if t < 2:
-                act(A("cq%d" % t), A("c%d" % t), AF.Identity, bias=1536.0)
+        if t < 2:
+            cp(A("kf%d" % t), A("e%d" % t))
+        if pas == 1 and t == 0:
+            act(A("cf0"), A("c0"))
+            act(A("cq0"), A("c0"), AF.Identity, bias=1536.0)
 
     def lists2(pas, kout):
         tt(A("w0"), A("j0"), A("j1"), OP.mult)
@@ -380,41 +423,50 @@ def rank_program(g, core, T, topo):
         tt(A("hi"), A("w1"), A("w0"), OP.subtract)
         cp(A("lou"), A("lo"))
         cp(A("hiu"), A("hi"))
-        for src, dst, co in (("lou", "glo", "cl"), ("hiu", "ghi", "ch")):
-            for gi in GI:
+        for gi in GI:
+            for src, dst, co in (("lou", "glo", "cl"), ("hiu", "ghi", "ch")):
                 ts(G(dst, gi, 16), IND(G("tri32", gi, 64), G(src, gi, 1)), -1536.0, OP.add)
                 if pas == 1:
                     act(G(co, gi, 16), IND(G("ck", gi, 64), G(src, gi, 1)))
-        for s, dst in enumerate(("lx", "ly")):
-            b = A("ps%d" % (2 + s), 0, 192)
-            mm(b, A("p%d0" % s), A("glo"), True, False)
-            mm(b, A("p%d1" % s), A("ghi"), False, True)
-            ts(A(dst), b, 1536.0, OP.add)
+        for gi in GI:
+            for s, dst in enumerate(("lx", "ly")):
+                b = "ps%d" % (2 + s + 4 * gi)
+                for u0, u1 in R2:
+                    n = 8 * (u1 - u0)
+                    for x, src in enumerate(("glo", "ghi") if group(u0) == gi else ()):
+                        for e in range(2):
+                            mm(A(b, 16 * u0 + n * x, 16 * u0 + n * x + n), A("p%d%d" % (s, e)),
+                               A(src, 16 * u0 + e, 16 * u1, 2), e == 0, e == 1)
+                ts(G(dst, gi, 16), A(b, 16 * GR[gi][0], 16 * GR[gi][1]), 1536.0, OP.add)
         for gi in GI:
             w = 64 * (GR[gi][1] - GR[gi][0])
             b = A("ps%d" % gi, 0, w)
-            mm(b, ONE1, A("kn", 0, w, p1=1), True, False)
+            mm(b, ONE1, A("km", 0, w, p1=1), True, False)
+            mm(b, A("gm1"), G("fl1", gi, 64), False, False)
+            mm(b, ONE1, A("kn", 0, w, p1=1), False, False)
             mm(b, A("gm"), G("fl0", gi, 64), False, False)
-            mm(b, A("gm2"), G("fl1", gi, 64), False, False)
             mm(b, A("ib"), G("phib", gi, 64), False, True)
             act(own(kout, *GR[gi]), b)
-        for gi in GI:
-            w = 64 * (GR[gi][1] - GR[gi][0])
-            if pas == 1:
-                b = A("ps4", 0, w)
-                mm(b, ONE1, A("kv", 0, w, p1=1), True, False)
-                mm(b, A("g3"), G("fl0", gi, 64), False, False)
-                mm(b, A("g2"), G("fl1", gi, 64), False, True)
-                act(G("lev", gi, 64), b)
 
     def round2(pas, kin, kout):
         tab = A("tab%d" % kin)
         now.update(step=kin, side=None)
         for u0, u1 in R2:
             gi = group(u0)
-            cuts = list(range(16 * u0, 16 * u1 + 1, 16))
-            if u0 == 0:
-                cuts.insert(1, 8)
+            cuts = [x for x in C2 if 16 * u0 <= x <= 16 * u1]
+            solo = SOLO if u1 == 12 else 0
+            x1 = 8 * (u0 + u1)
+            x0 = x1 - solo
+            if solo:
+                pair_gathers(tab, kin, "lx", "ly", [x for x in cuts if x < x0] + [x0])
+                cuts = [x for x in cuts if x >= x1]
+                pair_gathers(tab, kin, "lx", "ly", cuts[:AHEAD + 1])
+                cuts = cuts[AHEAD:]
+                act(A("ga", 16 * x0, 16 * x1), IND(tab, A("lx", x0, x1)), ext=kin)
+                act(A("zb", 0, 16 * solo), IND(tab, A("ly", x0, x1)), ext=kin)
+                mm(A("ps4", 0, 16 * solo), A("ib"), A("ga", 16 * x0, 16 * x1), True, False)
+                mm(A("ps4", 0, 16 * solo), A("nib"), A("zb", 0, 16 * solo), False, True)
+                act(A("db", 0, 16 * solo), A("ps4", 0, 16 * solo), AF.Relu)
             pair_gathers(tab, kin, "lx", "ly", cuts)
             n, c = 16 * (u1 - u0), 16 * (u0 - GR[gi][0])
             o = A("ps%d" % (5 + gi), c, c + n)
@@ -423,7 +475,15 @@ def rank_program(g, core, T, topo):
                 mm(o, A("i1k"), U("cl", u0, u1, 16), False, False)
                 mm(o, A("ni1k"), U("ch", u0, u1, 16), False, False)
             for r in range(16):
-                mm(o, A("gp" if r < 8 else "gn"), A("mn", 256 * u0 + r, 256 * u1, 16), False, r == 15)
+                x = 256 * u0 + 8 * n * (r // 8)
+                if r < 8 and solo:
+                    part = A(o[0], o[2] - 2 * solo, o[2])
+                    if 2 * solo < n:
+                        mm(A(o[0], o[1], part[1]), A("gp"), A("mn", x + r, 16 * x0, 8), False, False)
+                    mm(part, A("gp"), A("ga", 16 * x0 + r, 16 * x1, 8), False, False)
+                    mm(part, A("gn"), A("db", r, 16 * solo, 8), False, False)
+                else:
+                    mm(o, A("gp" if r < 8 else "gn"), A("mn", x + r % 8, x + 8 * n, 8), False, r == 15)
             for gi in ends(u1):
                 n = 16 * (GR[gi][1] - GR[gi][0])
                 scan(G("sc2", gi, 16), A("r16s", 0, n), A("ps%d" % (5 + gi), 0, n), OP.max)
@@ -434,22 +494,34 @@ def rank_program(g, core, T, topo):
                 send_done(kout, u1, S2)
         now.update(side=kout)
 
-    def places(kc):
+    def marks(t, tab, ext):
         for u in range(0, 12, 2):
-            (act if TG[u // 2] == "a" else cp)(U("mn", u, u + 2, 256), IND(A("tab%d" % kc), U("e0", u, u + 2, 16)), ext=kc)
-        now.update(side=kc + 2)
-        b = A("ps4", 0, 192)
-        mm(b, ONE1, A("kq", p1=1), True, False)
-        for r in range(16):
-            mm(b, A("dm", 128 * r, 128 * r + 128), A("mn", r, NW, 16), False, r == 15)
-        tt(A("tt"), b, A("qa"), OP.min)
-        tt(A("qa"), A("tt"), A("kf"), OP.max)
-        cp(A("f0"), A("qa"))
+            if t == 0 and u == LATE:
+                now.update(side=now["side"] + 1)
+            o = A("mn", NW * t + 256 * u, NW * t + 256 * u + 512)
+            (act if TG[t][u // 2] == "a" else cp)(o, IND(tab, U("e%d" % t, u, u + 2, 16)), ext=ext)
+            if TG[t][u // 2] in TG[t][:u // 2]:
+                ops[-1]["behind"] = len(ops) - 1 - u // 2 + TG[t].rindex(TG[t][u // 2], 0, u // 2)
+
+    def places(t):
+        for i, (u0, u1, _) in enumerate(LP):
+            b = A("ps%d" % (4 + i), 0, 16 * (u1 - u0))
+            mm(b, A("ih"), U("qh%d" % t, u0, u1, 16), True, False)
+            for r in range(16):
+                mm(b, A("dm", 128 * r, 128 * r + 128), A("mn", NW * t + 256 * u0 + r, NW * t + 256 * u1, 16), False, r == 15)
+            if i < 2:
+                place(t, i)
+
+    def place(t, i):
+        u0, u1, _ = LP[i]
+        tt(U("tq", u0, u1, 16), A("ps%d" % (4 + i), 0, 16 * (u1 - u0)), U("kf%d" % t, u0, u1, 16), OP.max)
+        ts(U("f%d" % t, u0, u1, 16), U("tq", u0, u1, 16), float(NONE if t else NEW[1] + NV - 1), OP.min)
 
     def level(pas, t, kin, kout):
-        tab = A("tab%d" % kin, 0, NW) if t else A("tab%d" % (kin - 1))
+        tab = A("tab%d" % (6 * pas + 3), 0, (NEW[1] + NV, NEW[1], NW)[t])
         need_p = not (pas == 0 and t == 0)
-        lst, c = "e%d" % t if t else "f0", "c%d" % t
+        lst, c = "e2" if t == 2 else "f%d" % t, "c%d" % t
+        ext = kin
         now.update(step=kin, side=kin)
         for u0, u1, halves in LP:
             n = 16 * (u1 - u0)
@@ -458,6 +530,14 @@ def rank_program(g, core, T, topo):
                 for m in range(m1 - m0):
                     mm(A("ps%d" % b, n * m, n * m + n), A("nib"), U(c, u0, u1, 16), False, False)
         now.update(side=None)
+
+        def opening(gi, h):
+            n = 16 * (GR[gi][1] - GR[gi][0])
+            if need_p:
+                mm(A("ps%d" % (3 + gi), 0, n), ONE33, A("kl", 0, n, p1=33), True, False)
+                mm(A("ps%d" % (3 + gi), 0, n), A("ib"), G(c, gi, 16), False, False)
+            mm(A("ps%d" % (5 + gi), 0, n), ONE1, A("kx", 0, n, p1=1), True, False)
+
         def part(name, i, m0, m1):
             u0, u1, _ = LP[i]
             return A(name, 128 * u0 + 16 * (u1 - u0) * m0, 128 * u0 + 16 * (u1 - u0) * m1)
@@ -468,20 +548,24 @@ def rank_program(g, core, T, topo):
 
         def fetch(i, h):
             u0, u1, halves = LP[i]
-            n, u = 16 * (u1 - u0), u0
-            while u < u1:
-                v = u + 1
-                while v < min(u1, u + 2) and LG[v] == LG[u]:
-                    v += 1
-                (act if LG[u] == "a" else cp)(U("ga", u, v, 256), IND(tab, U(lst, u, v, 16)), ext=kin)
-                u = v
+            n, x = 16 * (u1 - u0), 16 * u0
+            if t < 2 and i == 1:
+                last = max(j for j in range(len(ops)) if ops[j]["q"] == "v")
+                place(t, 2)
+                ops[-2]["behind"] = last
+            for e, cols in LG[i]:
+                (act if e == "a" else cp)(A("ga", 16 * x, 16 * (x + cols)), IND(tab, A(lst, x, x + cols)), ext=ext)
+                x += cols
             for b, m0, m1 in halves:
                 for r in range(2 * m0, 2 * m1):
                     x = n * (r // 2 - m0)
                     mm(A("ps%d" % b, x, x + n), A("ib"), A("ga", 256 * u0 + r, 256 * u1, 16), False, r == 2 * m1 - 1)
 
         def z(i, h):
-            act(part("zb", i, *LP[i][2][h][1:]), ebank(i, h), AF.Identity, bias=0.5)
+            if (i, h) in ZV:
+                ts(part("zb", i, *LP[i][2][h][1:]), ebank(i, h), 0.5, OP.add)
+            else:
+                act(part("zb", i, *LP[i][2][h][1:]), ebank(i, h), AF.Identity, bias=0.5)
 
         def dif(i, h):
             ms_ = LP[i][2][h][1:]
@@ -489,43 +573,71 @@ def rank_program(g, core, T, topo):
 
         def size(i, h):
             ms_ = LP[i][2][h][1:]
-            if i in ABS:
+            if (i, h) not in RELU:
                 act(part("ab", i, *ms_), part("db", i, *ms_), AF.Abs)
             else:
                 ts(part("ab", i, *ms_), part("db", i, *ms_), 0.0, OP.max)
 
-        def limit(i, h):
+        def bound(i, h):
             ms_ = LP[i][2][h][1:]
-            if i in THS:
-                act(part("tb", i, *ms_), part("zb", i, *ms_), AF.Relu, bias=A("thf"), scale=-2.0 ** -30)
-            else:
-                ts(part("tb", i, *ms_), part("zb", i, *ms_), float(2 ** 20), OP.is_lt, A("thf"), OP.mult)
+            if group(LP[i][0]) not in THC:
+                ts(part("tb", i, *ms_), part("zb", i, *ms_), float(2 ** 20), OP.is_lt, A("thf", 2, 3), OP.mult)
 
-        def sums(i, h):
+        def limit(gi, h):
+            if gi not in THC:
+                return
+            b = A("ps%d" % gi, 0, 64)
+            rows = [(i, m) for i in range(len(LP)) if group(LP[i][0]) == gi for m in range(8)]
+            for r, (i, m) in enumerate(rows):
+                mm(b, A("dm", 128 * r, 128 * r + 128), part("zb", i, m, m + 1), r == 0, r == len(rows) - 1)
+            ts(A("vf", 64 * gi, 64 * gi + 64), b, 2.0 ** -30, OP.is_lt)
+
+        def sums(i, h, turn=False):
             u0, u1, halves = LP[i]
             gi = group(u0)
             n, o = 16 * (u1 - u0), 16 * (u0 - GR[gi][0])
             _, m0, m1 = halves[h]
             tb, xb = A("ps%d" % (3 + gi), o, o + n), A("ps%d" % (5 + gi), o, o + n)
-            terms = (("xn", "tb"), ("xp", "ab")) if i in ABS else (("xn", "tb"), ("xn", "db"), ("xp2", "ab"))
-            if need_p:
-                if h == 0:
-                    mm(tb, ONE33, A("kl", 0, n, p1=33), True, False)
-                    mm(tb, A("ib"), U(c, u0, u1, 16), False, False)
-                for m in range(m0, m1):
-                    mm(tb, A("lu"), part("db", i, m, m + 1), False, m == 7)
-            if t == 1 and h == 0:
-                mm(xb, ONE1, A("kx", 0, n, p1=1), True, False)
+            terms = (("xn", "db"), ("xp2", "ab")) if (i, h) in RELU else (("xp", "ab"),)
+            if turn:
+                if need_p:
+                    for m in range(m0, m1):
+                        mm(tb, A("lu"), part("db", i, m, m + 1), False, m == 7 and bool(ends(u1)))
+                    if m1 == 8:
+                        for gi in ends(u1):
+                            phases(t, gi)
+                return
+            last = m1 == 8 and bool(ends(u1))
+            if gi not in THC:
+                terms = (("xn", "tb"),) + terms
+            if last and gi in THC:
+                for x in range(0, o + 1, 64):
+                    for l in ("th", "tl"):
+                        mm(A(xb[0], x, x + 64), A(l + str(x // 64)), A("vf", 64 * gi, 64 * gi + 64), False, False)
             for j, (l, r) in enumerate(terms):
                 for m in range(m0, m1):
-                    mm(xb, A(l), part(r, i, m, m + 1), t != 1 and j == 0 and m == 0, j == len(terms) - 1 and m == 7)
+                    mm(xb, A(l), part(r, i, m, m + 1), False, last and j == len(terms) - 1 and m == 7)
             if m1 == 8:
                 for gi in ends(u1):
                     finish(pas, t, kout, gi)
 
-        call = {"f": fetch, "z": z, "d": dif, "a": size, "l": limit, "s": sums}
+        call = {"f": fetch, "z": z, "d": dif, "a": size, "l": limit, "s": sums, "b": bound, "o": opening,
+                "t": lambda i, h: sums(i, h, True)}
         for w in LO.split():
+            if t < 2:
+                for f in later.pop(w, []):
+                    n = len(ops)
+                    f()
+                    ops[n]["behind"] = max(j for j in range(n) if ops[j]["q"] == ops[n]["q"] and ops[j]["side"] is None)
             call[w[0]](int(w[1]), int(w[2:] or 0))
+
+    def phases(t, gi):
+        tb = A("ps%d" % (3 + gi), 0, 16 * (GR[gi][1] - GR[gi][0]))
+        if gi in ZZV:
+            ts(G("zz", gi, 16), tb, -1663.5, OP.add)
+        else:
+            act(G("zz", gi, 16), tb, AF.Identity, bias=-1663.5)
+        tt(G("rr%d" % t, gi, 16), tb, G("zz", gi, 16), OP.subtract)
 
     def finish(pas, t, kout, gi):
         n = 16 * (GR[gi][1] - GR[gi][0])
@@ -533,43 +645,50 @@ def rank_program(g, core, T, topo):
         su = G("su%d" % t, gi, 1)
 
         def h(name):
-            return G(name, gi, 16)
-        if pas == 1 or t > 0:
-            act(h("zz"), tb, AF.Identity, bias=-1663.5)
-            tt(h("rr"), tb, h("zz"), OP.subtract)
-        if t == 2:
-            ts(h("pb"), h("rr"), -1536.0, OP.add)
-            ts(h("mk"), xb, 0.0, OP.is_gt, MARK, OP.mult)
-            tt(IND(own(kout, *GR[gi]), su), h("pb"), h("mk"), OP.add)
-            send_done(kout, GR[gi][1], SL)
-        if t == 1:
-            o = NW + 192 * rank
-            ts(h("pb"), xb, MARK, OP.min, -1536.0, OP.max)
-            tt(A("tab%d" % (kout - 1), o + 16 * GR[gi][0], o + 16 * GR[gi][1]), h("rr"), h("pb"), OP.add)
-            if GR[gi][1] == 12:
-                send(kout, A("tab%d" % (kout - 1), o, o + 192))
+            return G(name + (str(t) if name in ("rr", "mk", "nk") else ""), gi, 16)
         if t > 0:
+            o = NEW[t] + 192 * rank
+            new = A("tab%d" % (6 * pas + 3), o + 16 * GR[gi][0], o + 16 * GR[gi][1])
+            ts(h("pb"), xb, MARK, OP.min, -1536.0, OP.max)
+            tt(new, h("rr"), h("pb"), OP.add)
+            if GR[gi][1] == 12:
+                send(kout, A(new[0], o, o + 192))
             now.update(side=kout)
-        if pas == 1 or t == 0:
+        if t == 0:
             ts(h("nk"), xb, 0.0, OP.is_le)
+        elif pas == 1:
+            ts(h("nk"), xb, 0.0, OP.is_le, 512.0, OP.mult)
         if pas == 0:
             if t == 0:
                 tt(IND(own(6, *GR[gi]), su), h("ag0"), h("nk"), OP.mult)
                 send_done(kout, GR[gi][1], SL)
                 now.update(side=kout)
-            if t < 2:
-                ts(h("mk"), xb, 0.0, OP.is_gt, MARK, OP.mult)
-            tt(IND(G("ck", gi, 64), su), h("jv%d" % t), h("mk"), OP.mult)
-        else:
-            if t == 2:
-                tt(h("dd"), h("pb"), h("c%d" % t), OP.subtract)
+            ts(h("mk"), xb, 0.0, OP.is_gt, MARK, OP.mult)
+            if t == 2 and gi in CKG:
+                later[GAP].append(lambda: tt(IND(G("ck", gi, 64), su), h("jv2"), h("mk"), OP.mult))
+            elif t == 2:
+                now.update(side=kout + CKW)
+                tt(IND(G("ck", gi, 64), su), h("jv2"), h("mk"), OP.mult)
             else:
-                tt(h("dd"), h("rr"), h("cq%d" % t), OP.subtract)
+                tt(IND(G("ck", gi, 64), su), h("jv%d" % t), h("mk"), OP.mult)
+        elif t == 0:
+            tt(h("dd"), h("rr"), h("cq0"), OP.subtract)
             tt(h("tt"), h("dd"), h("nk"), OP.mult)
-            tt(IND(G("pout", gi, 64), su), h("tt"), h("cf%d" % t), OP.add)
-            if t == 0:
-                store(T.yphi[:, 64 * GR[gi][0]:64 * GR[gi][1]], G("pout", gi, 64), "d_y%d" % gi)
+            tt(IND(G("pout", gi, 64), su), h("tt"), h("cf0"), OP.add)
+            store(T.yphi[:, 64 * GR[gi][0]:64 * GR[gi][1]], G("pout", gi, 64), "d_y%d" % gi)
         now.update(side=None)
+
+    def record(t):
+        b = A("ps%d" % (2 if t == 2 or R1 else 3), 0, 192)
+        mm(b, A("ib"), A("c%d" % t), True, False)
+        mm(b, A("ib"), A("nk%d" % t), False, True)
+        tt(A("tq%d" % t), b, A("tab9", NEW[t] + 192 * rank, NEW[t] + 192 * rank + 192), OP.min)
+        for gi in GI[:3 - t]:
+            put(t, gi)
+
+    def put(t, gi):
+        cp(IND(G("pout", gi, 64), G("su%d" % t, gi, 1)), G("tq%d" % t, gi, 16))
+        ops[-1]["cap"] = len(ops)
 
     for pas in range(2):
         k = 6 * pas
@@ -580,23 +699,39 @@ def rank_program(g, core, T, topo):
         prep_level(pas, 1)
         round2(pas, k + 2, k + 3)
         prep_level(pas, 2)
-        for gi in GI:
-            act(own(k + 4, *GR[gi]), own(k + 3, *GR[gi]))
         if pas == 1:
             for gi in GI:
-                cp(IND(G("lev", gi, 64), G("su2", gi, 1)), A("l2", 0, 16 * (GR[gi][1] - GR[gi][0])))
+                w = 64 * (GR[gi][1] - GR[gi][0])
+                b = A("ps%d" % (5 + gi), 0, w)
+                mm(b, ONE1, A("kv", 0, w, p1=1), True, False)
+                mm(b, A("g3"), G("fl0", gi, 64), False, False)
+                mm(b, A("g2"), G("fl1", gi, 64), False, False)
+                mm(b, A("i70"), own(k + 3, *GR[gi]), False, True)
+                act(G("lev", gi, 64), b, AF.Relu)
             rec("s", lambda: g.sync.dma_start(T.ylev[:], T.lev[0:128:16, :]), [], [A("lev")], 0.1, sem="d_lev", lag=LAT)
+        later[GAP] = [lambda: record(2)] if pas else []
         level(pas, 2, k + 3, k + 4)
         now.update(side=k + 4)
-        places(k + 3)
+        marks(1, A("tab%d" % (k + 3), 0, NW), k + 3)
+        places(1)
+        marks(0, A("tab%d" % (k + 3), 0, NW), k + 3)
         level(pas, 1, k + 4, k + 5)
+        now.update(side=k + 5)
+        places(0)
         if pas == 0:
-            now.update(side=5)
+            later[GAP], later["o0"] = [], []
             for gi in GI:
                 b = A("ps%d" % (3 + gi), 0, 64 * (GR[gi][1] - GR[gi][0]))
-                mm(b, A("ib"), own(0, *GR[gi]), True, False)
-                mm(b, A("ib"), G("ck", gi, 64), False, True)
-                act(own(6, *GR[gi]), b, AF.Relu)
+                later["o0"].append(lambda gi=gi, b=b: (mm(b, A("ib"), own(0, *GR[gi]), True, False),
+                                                       mm(b, A("ib"), G("ck", gi, 64), False, True)))
+                later[GAP].append(lambda gi=gi, b=b: ts(own(6, *GR[gi]), b, 0.0, OP.max))
+        elif R1:
+            later[GAP] = [lambda: record(1)]
+        else:
+            last = max(j for j in range(len(ops)) if ops[j]["q"] == "v")
+            record(1)
+            ops[-3]["behind"] = last
+            later[GAP] = [lambda: put(2, 1)]
         level(pas, 0, k + 5, k + 6)
 
     emit(g, T, ops, sends, per_send)
@@ -628,10 +763,12 @@ def emit(g, T, ops, sends, per_send):
                 h.append((d[1], d[2], i, w))
         for j in deps:
             after[j] = HOP if ops[j]["sem"] == "none" else ops[j]["lag"]
-        if o["ext"] is not None:
-            js = sends[o["ext"]]
+        for k in o["ext"]:
+            js = sends[k]
             for n, j in enumerate(js):
-                after[j] = LAT + sum(ops[x]["lag"] for x in js[n:])
+                after[j] = WAY + sum(ops[x]["lag"] for x in js[n:])
+        if "behind" in o:
+            after.setdefault(o["behind"], 0.0)
         o["deps"], o["after"], o["succ"] = deps, after, []
     allsends = sorted(j for js in sends.values() for j in js)
     for a, b in zip(allsends[:-1], allsends[1:]):
@@ -643,7 +780,7 @@ def emit(g, T, ops, sends, per_send):
         o["due"] = o["step"] if o["side"] is None else min([99] + [ops[s]["due"] for s in o["succ"]])
     for i in range(len(ops) - 1, -1, -1):
         o = ops[i]
-        o["rank"] = i if o["side"] is None else min([len(ops)] + [ops[s]["rank"] for s in o["succ"]])
+        o["rank"] = i if o["side"] is None else min([o.get("cap", len(ops))] + [ops[s]["rank"] for s in o["succ"]])
     closing = {js[-1]: k for k, js in sends.items() if k < 12}
     owed, todo = {}, {}
     opening = {}
@@ -652,11 +789,11 @@ def emit(g, T, ops, sends, per_send):
             opening.setdefault(o["step"], i)
     for o in ops:
         if o["side"] is not None:
-            o["urgent"] = o["rank"] < opening.get(o["due"], 0) + 8
+            o["urgent"] = o["rank"] < len(ops) and bool(ops[o["rank"]]["ext"])
             owed[o["q"], o["due"]] = owed.get((o["q"], o["due"]), 0) + o["urgent"]
         else:
             todo[o["q"], o["step"]] = todo.get((o["q"], o["step"]), 0) + 1
-    sent, end = -1, LAT + 0.5
+    sent, end = -1, LAT - 0.3
     free = {q: 0.0 for q in "vapgs"}
     done = {q: 0.0 for q in "vapgs"}
     left = [len(o["after"]) for o in ops]
@@ -677,11 +814,11 @@ def emit(g, T, ops, sends, per_send):
                 o = ops[j]
                 if o["q"] == q and o["side"] is not None and min(o["side"], o["due"]) <= pause:
                     s = max(free[q], ready[j])
-                    fits = s + o["cost"] <= min(at, limit) + HOP
+                    fits = s + o["cost"] <= min(at, limit + (q in "gp")) + HOP
                     if o["due"] <= pause:
-                        ok = s <= at and (fits or pick is None or o["rank"] < pick)
+                        ok = s <= at and (s + o["cost"] <= at + HOP or pick is None or o["rank"] < pick)
                     else:
-                        ok = fits and not owed.get((q, pause))
+                        ok = fits and (pause < 1 or not owed.get((q, pause)))
                     if ok or pause == 12:
                         fill.append((round(s, 1), o["rank"], j))
             if fill and min(fill)[0] <= at:
@@ -698,7 +835,7 @@ def emit(g, T, ops, sends, per_send):
             todo[q, ops[i]["step"]] -= 1
             done[q] = free[q]
         if i in closing:
-            sent, end = closing[i], start + ROOM * (1 if closing[i] else 2)
+            sent, end = closing[i], start + ROOM * (1 if closing[i] else ROOM0)
         order.append(i)
         for s in ops[i]["succ"]:
             left[s] -= 1
@@ -711,8 +848,8 @@ def emit(g, T, ops, sends, per_send):
         place[i] = n
         kn = known[o["q"]]
         waits = []
-        if o["ext"] is not None:
-            s, v = "arr%d" % o["ext"], per_send * len(sends[o["ext"]])
+        for k in o["ext"]:
+            s, v = "arr%d" % k, per_send * len(sends[k])
             if kn.get(s, 0) < v:
                 waits.append((s, v))
                 kn[s] = v

from concourse.bass import DstId, RemoteDMATransfer
from concourse.mybir import AluOpType, ActivationFunctionType, AxisListType

NV, NW = 768, 3072
GR = [(0, 8), (8, 12)]
FIRST = [(0, 6), (6, 12)]
SR = [(0, 4), (4, 8), (8, 12)]
GAP = "t1"
T6V = ()
R1 = 0
CKG = (0,)
CKW = 0
WAY = 2.0
C1 = [0, 16, 48, 64, 96, 128, 160, 192, 224, 256, 288, 320, 352, 372, 384]
SOLO = 16
AHEAD = 0
LATE = 0
CAP6 = 60
C2 = [0, 16, 48, 64, 96, 128, 144, 160, 176, 192]
EARLY = 0.5
ONCE = 2.5
ROOM0 = 2.5
ROOM = 2.0
S2 = [(0, 8), (8, 12)]
SL = [(0, 12)]
RP = [(0, 2), (2, 4), (4, 6), (6, 8), (8, 10), (10, 11), (11, 12)]
R2 = [(0, 4), (4, 8), (8, 12)]
LP = [(0, 4, [(0, 0, 8)]), (4, 8, [(1, 0, 8)]), (8, 12, [(2, 0, 4), (7, 4, 8)])]
LG = [[("a", 28), ("v", 36)], [("a", 32), ("v", 32)], [("a", 24), ("v", 40)]]
THC = (0,)
LO = "f0 f1 f2 o0 o1 z0 z1 d0 z20 d1 z21 a0 d20 a1 d21 t0 b20 b21 l0 t1 s0 s1 a20 a21 t20 t21 s20 s21"
TG = {0: "avavaa", 1: "avavaa"}
NEAR = 4
RELU = ()
ZV = ()
ZZV = ()
OFF = 1088.0
MARK = float(2 ** 42)
MARK2 = float(2 ** 70)
NEW = {2: 4096, 1: 5120}
NONE = NEW[2] + NV
BF, F16, F32, I32, U16 = "bfloat16", "float16", "float32", "int32", "uint16"

SCRATCH = {}
PART = {}


def _sb(dt, cols, names):
    for n in names.split():
        SCRATCH[n] = ("sbuf", [128, cols], dt)


def _pack(base, dt, cols, names):
    step = max(cols, 16)
    for i, n in enumerate(names.split()):
        PART[n] = (base, step * i, cols)
    _sb(dt, step * len(names.split()), base)


_sb(I32, NV, "amp32 phi32 tri32 tq32")
_sb(I32, 1, "th32")
_sb(F32, 8, "thf")
_sb(BF, 8, "thb")
_sb(F32, 16, "srow")
_sb(BF, NW, "tab0 tab1 tab2 tab6 tab7 tab8")
_sb(BF, NEW[1] + NV, "tab3 tab9")
_sb(BF, 6144, "ga mn")
_sb(BF, 1536, "zb db ab tb")
_sb(U16, 384, "offa offb")
_pack("l192", U16, 192, "lx ly e0 e1 e2 f0 f1")
_sb(F16, NV, "r16 x1 xa xb sf")
_sb(F32, NV, "scn pout lev")
_sb(BF, NV, "phib fl0 fl1 ck")
_pack("h192", F16, 192, "glo ghi rr0 rr1 rr2 qh0 qh1")
_pack("b192", BF, 192, "c0 c1 c2 ag0 jv0 jv1 jv2 cl ch zz pb mk0 mk1 mk2 nk0 nk1 nk2 dd bd")
_pack("f192", F32, 192, "cf0 cq0 tt tq tq1 tq2 r16s sc2 kf0 kf1")
_sb(F32, 128, "r64")
_sb(BF, 512, "ke km kn kv jc pick")
_sb(BF, 2048, "dm")
_pack("b128", BF, 128, "oneb ib nib i8 i20 i1k ni1k gt gp gn xp xp2 xn g1n g512 g3 g2 gm gm1 i70 b1 lu s64 ks ku kl kb kx mark"
      " th0 th1 tl0 tl1 vf")
_pack("h128", F16, 128, "p00 p01 p10 p11 gh s32 ih")
_pack("smi", I32, 12, "mi si0 si1 si2 j0 j1 io0 io1")
_pack("smu", U16, 12, "su0 su1 su2 lou hiu")
_pack("smf", F32, 12, "w0 w1 w2 lo hi y2 base")
for _i in range(8):
    SCRATCH["ps%d" % _i] = ("psum", [128, 512], F32)

SEMAPHORES = (["sv", "sa", "sp", "sg", "sent", "d_a0", "d_a1", "d_tri", "d_phi", "d_th", "d_y0", "d_y1", "d_lev"]
              + ["arr%d" % i for i in range(12)])
QSEM = {"v": "sv", "a": "sa", "p": "sp", "g": "sg"}
OP = AluOpType
AF = ActivationFunctionType
COSTS = (0.0009, 1.56, 3.8, 0.0005, 0.1, 2.5, 0.045, 0.00005)
CYC, GAT, SCA, PEC, HOP, LAT, ROW, BYTE = COSTS


def A(name, c0=0, c1=None, step=1, p0=0, p1=128):
    if name in PART:
        base, o, cols = PART[name]
        return (base, o + c0, o + (cols if c1 is None else c1), step, p0, p1)
    if c1 is None:
        c1 = SCRATCH[name][1][1]
    return (name, c0, c1, step, p0, p1)


def IND(win, off):
    return ("*", win, off)


def width(d):
    return 16 * (d[2][2] - d[2][1]) if d[0] == "*" else (d[2] - d[1] + d[3] - 1) // d[3]


def narrow(*ds):
    return all(SCRATCH[d[0]][2] in (BF, F16, U16) for d in ds)


def rank_program(g, core, T, topo):
    rank = T.rank_of(core)
    if rank is None:
        return
    ops = []
    now = {"step": -1, "side": None}

    def ap(d):
        if not isinstance(d, tuple):
            return d
        if d[0] == "*":
            return ap(d[1]).indirect(ap(d[2]))
        n, c0, c1, st, p0, p1 = d
        t = T[n]
        if p0 == 0 and p1 == 128:
            return t[:, c0:c1] if st == 1 else t[:, c0:c1:st]
        return t[p0:p1, c0:c1] if st == 1 else t[p0:p1, c0:c1:st]

    def rec(q, fn, outs, ins, cost, ext=None, sem=None, lag=HOP):
        rd, wr = [], []
        for d in outs:
            if d[0] == "*":
                wr.append(d[1]); rd.append(d[2])
            else:
                wr.append(d)
        for d in ins:
            if isinstance(d, tuple):
                if d[0] == "*":
                    rd.append(d[1]); rd.append(d[2])
                else:
                    rd.append(d)
        ext = () if ext is None else ext if isinstance(ext, tuple) else (ext,)
        ops.append({"q": q, "fn": fn, "rd": rd, "wr": wr, "ext": ext, "sem": sem, "cost": cost, "lag": lag, **now})

    def dur(o, i, per=None):
        if i is not None and i[0] == "*":
            return 0.06 + GAT * CYC * width(i)
        if o[0] == "*":
            return 0.05 + SCA * CYC * width(o)
        if per is None:
            per = 0.5 if narrow(o, i or o) else 1.0
        return CYC * max(64, per * width(o))

    def cp(o, i, ext=None):
        rec("v", lambda: g.vector.tensor_copy(ap(o), ap(i)), [o], [i], dur(o, i), ext)

    def tt(o, a, b, op, ext=None):
        per = 1.0 if a[0].startswith("ps") else 2.0
        rec("v", lambda: g.vector.tensor_tensor(ap(o), ap(a), ap(b), op), [o], [a, b], dur(o, a, per), ext)

    def ts(o, a, s1, op0, s2=None, op1=None):
        if op1 is None:
            rec("v", lambda: g.vector.tensor_scalar(ap(o), ap(a), ap(s1), None, op0), [o], [a, s1], dur(o, a))
        else:
            rec("v", lambda: g.vector.tensor_scalar(ap(o), ap(a), ap(s1), ap(s2), op0, op1), [o], [a, s1, s2], dur(o, a))

    def ms(o, val):
        rec("v", lambda: g.vector.memset(ap(o), val), [o], [], dur(o, None))

    def scan(o, d0, d1, op1):
        rec("v", lambda: g.vector.tensor_tensor_scan(ap(o), ap(d0), ap(d1), 0.0, OP.add, op1), [o], [d0, d1], dur(o, d1))

    def act(o, i, func=AF.Copy, bias=0.0, scale=1.0, ext=None):
        rec("a", lambda: g.scalar.activation(ap(o), ap(i), func, bias=ap(bias), scale=ap(scale)), [o], [i, bias, scale],
            dur(o, i, 1.0), ext)

    def mm(o, l, r, start, stop):
        rec("p", lambda: g.tensor.matmul(ap(o), ap(l), ap(r), start, stop), [o], [l, r], PEC * max(64, width(r)))

    def sel(o, i, pat, cmp, fill, base, cm):
        rec("g", lambda: g.affine_select(ap(o), ap(i), pat, cmp, fill, base, cm), [o], [i], 0.17 + 2 * CYC * width(o))

    def iota(o, pat, base, cm):
        rec("g", lambda: g.iota(ap(o), pat, base, cm), [o], [], 0.13 + 2 * CYC * width(o))

    def load(q, o, src, sem):
        e = g.sync if q == "s" else g.scalar
        rec(q, lambda: e.dma_start(ap(o), src), [o], [], 0.1, sem=sem, lag=LAT + 32 * BYTE * width(o))

    def store(dst, i, sem):
        rec("s", lambda: g.sync.dma_start(dst, ap(i)), [], [i], 0.1, sem=sem, lag=LAT)

    peers = [c for c in T.cores if c != core]
    near = [c for c in peers if c in topo.cores_of(core)]
    far = [c for c in peers if c not in near]
    off_eng = topo.engines(core, far[0])
    on_eng = [e for e in topo.engines(core, near[0]) if e not in off_eng]
    on_eng = on_eng[::len(on_eng) // NEAR]
    share = len(off_eng) // len(far)
    masks = {near[0]: sum(1 << e for e in on_eng)}
    for i, c in enumerate(far):
        masks[c] = sum(1 << e for e in off_eng[i * share:(i + 1) * share])
    per_send = len(on_eng) + share * len(far)
    sends, later = {}, {}

    def own(k, u0=0, u1=12):
        return A("tab%d" % k, rank * NV + 64 * u0, rank * NV + 64 * u1)

    def send(k, d):
        def fn():
            trs = []
            for c in far + near:
                rid, pid = topo.addr(c, core)
                trs.append(RemoteDMATransfer(dst_ids=[DstId(rid=rid, pnc=pid)], dma_engine_mask=masks[c],
                                             remote_sem=T.sem["arr%d" % k], src=ap(d), dst=ap(d)))
            g.remote_dma_fused(trs, local_sem=T.sem.sent)
        sends.setdefault(k, []).append(len(ops))
        rec("g", fn, [], [d], 0.3 if k else ONCE, sem="none", lag=128 // share * (ROW + 2 * BYTE * width(d)))

    def send_done(k, u1, parts):
        for a, b in parts:
            if b == u1:
                send(k, own(k, a, b))

    def U(name, u0, u1, per):
        return A(name, per * u0, per * u1)

    def G(name, gi, per):
        return U(name, GR[gi][0], GR[gi][1], per)

    def group(u):
        return [gi for gi, (a, b) in enumerate(GR) if a <= u < b][0]

    def ends(u1):
        return [gi for gi, (a, b) in enumerate(GR) if b == u1]

    GI = range(len(GR))
    ONE33, ONE1 = A("oneb", p1=33), A("oneb", p1=1)
    B16 = A("b1", p1=16)
    DOWN = OFF - 31.0 / 64

    for i, (u0, u1) in enumerate(FIRST):
        load("sa"[i], U("amp32", u0, u1, 64), T.amp[:, 64 * u0:64 * u1], "d_a%d" % i)
    load("s", A("tri32"), T.tri[:], "d_tri")
    load("s", A("phi32"), T.phi[:], "d_phi")
    load("s", A("th32"), T.th[:], "d_th")
    for u0, u1 in FIRST:
        cp(own(0, u0, u1), U("amp32", u0, u1, 64))
    send(0, own(0))
    now.update(side=-1)
    ms(A("oneb"), 1.0)
    for s in range(2):
        for e in range(2):
            o = A("pick", 256 * s + 128 * e, 256 * s + 128 * e + 128)
            sel(o, A("oneb"), [[-16, 8], [200 - 400 * e, 2], [-2, 8]], OP.is_equal, 0.0, 200 * e - s, 1)
            cp(A("p%d%d" % (s, e)), o)
    sel(A("ib"), A("oneb"), [[-1, 128]], OP.is_equal, 0.0, 0, 1)
    sel(B16, A("oneb", p1=16), [[0, 8], [-1, 16]], OP.is_equal, 0.0, 0, 1)
    sel(A("gt"), A("oneb"), [[-16, 8], [0, 16]], OP.is_ge, 0.0, 0, 1)
    sel(A("gt"), A("gt"), [[16, 8], [0, 16]], OP.is_ge, 0.0, 15, -1)
    for j in range(4):
        ms(A("kb", j, 128, 4, p1=16), -j / 4.0)
        ms(A("jc", j, 512, 4), (j - 4) * 2.0 ** 16 / MARK)
    sel(A("kb", p1=16), A("kb", p1=16), [[0, 2], [-1, 16], [0, 4]], OP.is_equal, -float(2 ** 22), 0, 1)
    ms(A("bd", p1=16), 0.0)
    sel(A("bd", p1=16), A("bd", p1=16), [[0, 12], [-1, 16]], OP.is_equal, -2 * MARK, 0, 1)
    iota(A("io0"), [[0, 12]], 0, 4)
    for gi in GI:
        iota(G("io1", gi, 1), [[64, GR[gi][1] - GR[gi][0]]], 0, 0)
    ts(A("io0"), A("io0"), 63, OP.bitwise_and)
    tt(A("base"), A("io0"), A("io1"), OP.add)
    for n, a, b in (("ks", OFF, -31.0 / 64), ("ku", OFF - 8192, -31.0 / 64), ("kl", 50688.0, -63.0 / 128)):
        ms(A(n, p1=64), 0.0)
        ms(A(n, p1=1), a)
        ms(A(n, p0=32, p1=33), b)
    for n, a in (("ke", 49152.0), ("kv", -57.0), ("kn", 16 * MARK), ("kx", -2 * MARK), ("km", 20 * MARK2)):
        ms(A(n, p1=1), a)
    ms(A("r64"), 0.0)
    ms(A("r64", 0, 128, 64), -float(2 ** 26))
    ms(A("r16s"), 0.0)
    ms(A("r16s", 0, 192, 16), -4 * MARK)
    ms(A("ck"), 0.0)
    ts(A("r16"), A("tri32"), -1536.0, OP.add)
    for s, dst in enumerate(("offa", "offb")):
        for e in range(2):
            mm(A("ps%d" % (6 + s), 0, 384), A("p%d%d" % (s, e)), A("r16", e, NV, 2), e == 0, e == 1)
        ts(A(dst), A("ps%d" % (6 + s), 0, 384), 1536.0, OP.add)
    mm(A("ps5", 0, 128), B16, B16, True, True)
    ts(A("s32"), A("ps5", 0, 128), 1.0 / 32, OP.mult)
    ts(A("s64"), A("ps5", 0, 128), 1.0 / 64, OP.mult)
    ts(A("srow"), A("ps5", 0, 16), 4096 / MARK2, OP.mult)
    cp(A("ih"), A("ib"))
    for n, f in (("i8", 0.125), ("nib", -1.0), ("i20", 2.0 ** 20), ("i1k", 1024.0), ("ni1k", -1024.0),
                 ("i70", -1 / MARK2)):
        ts(A(n), A("ib"), f, OP.mult)
    for n, f in (("gh", -1.0), ("g1n", -1.0), ("g512", 512.0), ("gp", 1024.0), ("gn", -1024.0), ("xp", 4 * MARK),
                 ("xp2", 8 * MARK), ("xn", -4 * MARK), ("gm", -MARK), ("gm1", -1.25 * MARK2), ("g3", 3.0), ("g2", 0.75)):
        ts(A(n), A("gt"), f, OP.mult)
    tt(A("lu"), A("s64"), A("i8"), OP.add)
    cp(A("phib"), A("phi32"))
    cp(A("thb", 0, 1), A("th32"))
    cp(A("thf", 2, 3), A("th32"))
    mm(A("ps4", 0, 1), A("gt"), A("thb", 0, 1), True, True)
    cp(A("thb", 1, 2), A("ps4", 0, 1))
    tt(A("thb", 2, 3), A("ps4", 0, 1), A("thb", 1, 2), OP.subtract)
    rec("v", lambda: g.vector.tensor_reduce(ap(A("thf", 0, 1)), ap(A("s64", 0, 8)), AxisListType.X, OP.add),
        [A("thf", 0, 1)], [A("s64", 0, 8)], 64 * CYC)
    ts(A("thf", 1, 2), A("thf", 0, 1), -1.0, OP.mult, 1.0 / 64, OP.add)
    for h in range(2):
        for c, n in ((1, "th"), (2, "tl")):
            ts(A("thf", 2 + 2 * h + c, 3 + 2 * h + c), A("thf", h, h + 1), A("thb", c, c + 1), OP.mult, 64.0, OP.mult)
            ts(A(n + str(h)), A("xn"), A("thf", 2 + 2 * h + c, 3 + 2 * h + c), OP.mult)
    ts(A("tq32"), A("tri32"), 2, OP.arith_shift_right)
    for r in range(16):
        act(A("dm", 128 * r, 128 * r + 128), A("ib"), AF.Identity, scale=A("srow", r, r + 1))
    for k in (3, 9):
        ms(A("tab%d" % k, NW, NEW[2]), MARK)
        ms(A("tab%d" % k, NONE, NEW[1]), MARK)
    ms(A("mark"), MARK2)
    act(A("pout"), A("phib"))

    def pair_gathers(tab, k, la, lb, cuts):
        for x0, x1 in zip(cuts[:-1], cuts[1:]):
            (act if x0 else cp)(A("ga", 16 * x0, 16 * x1), IND(tab, A(la, x0, x1)), ext=k)
            tt(A("mn", 16 * x0, 16 * x1), IND(tab, A(lb, x0, x1)), A("ga", 16 * x0, 16 * x1), OP.min, ext=k)

    def round01(pas, t, kin, kout):
        tab = A("tab%d" % kin)
        ain, aout = ("xb", "xa") if t == 0 else ("xa", "xb")

        def fl(u0, u1):
            return U("fl%d" % t, u0, u1, 64)
        now.update(step=kin, side=kin)
        if t == 0:
            act(A(ain), own(kin), AF.Identity, bias=OFF)
        now.update(side=None)
        for i, (u0, u1) in enumerate(RP):
            w = 64 * (u1 - u0)
            last = u1 == 12
            cuts = [x for x in C1 if 32 * u0 <= x <= 32 * u1]
            pair_gathers(tab, kin, "offa", "offb", cuts)
            sb, kb, ub = (A("ps%d" % b, 0, w) for b in (i % 3, 3 + i % 2, 5 + i % 3))

            def pc(n):
                return U(n, u0, u1, 64)

            def trip(m):
                return A("mn", 512 * u0 + m, 512 * u1, 8)
            mm(kb, B16, A("kb", 0, w, p1=16), True, False)
            if t == 1:
                mm(kb, A("i20"), pc("fl0"), False, False)
            if pas == 1:
                mm(kb, A("nib"), pc("ck"), False, False)
            if last:
                for m in range(8):
                    mm(kb, A("g1n"), trip(m), False, m == 7)

            def choose():
                scan(pc("scn"), A("r64", 0, w), kb, OP.max)
                for u in range(u0, u1):
                    act(fl(u, u + 1), A(kb[0], 64 * (u - u0), 64 * (u - u0) + 64), AF.Sign, scale=-1.0,
                        bias=A("scn", 64 * u + 63, 64 * u + 64))
            if last:
                choose()
            mm(sb, ONE33, A("ks", 0, w, p1=33), True, False)
            for m in range(8):
                mm(sb, A("i8"), trip(m), False, m == 7)
            act(pc("sf"), sb, AF.Identity, bias=-8 * DOWN, scale=8.0)
            tt(pc("x1"), sb, pc(ain), OP.min)
            if not last:
                mm(kb, A("gh"), pc("sf"), False, True)
            mm(ub, ONE33, A("ku", 0, w, p1=33), True, False)
            mm(ub, A("s32"), pc("sf"), False, False)
            if not last:
                choose()
            mm(ub, A("g512"), fl(u0, u1), False, True)
            tt(pc(aout), ub, pc("x1"), OP.min)
            if last:
                ts(own(kout, u0, u1), pc(aout), -OFF, OP.add, 0.0, OP.max)
            else:
                act(own(kout, u0, u1), pc(aout), AF.Relu, bias=-OFF)
            send_done(kout, u1, SR)
        now.update(side=kout)
        ts(A("mi"), A("scn", 63, NV, 64), -4.0, OP.mult)
        ts(A("j%d" % t), A("mi"), 3, OP.bitwise_and)
        tt(A("si%d" % t), A("j%d" % t), A("base"), OP.add)
        cp(A("su%d" % t), A("si%d" % t))

    def prep_level(pas, t):
        for gi in GI:
            su = G("su%d" % t, gi, 1)
            cp(G("e%d" % t, gi, 16), IND(G("tri32", gi, 64), su))
            if t < 2:
                cp(G("qh%d" % t, gi, 16), IND(G("tq32", gi, 64), su))
            act(G("c%d" % t, gi, 16), IND(G("phib", gi, 64), su))
            if pas == 0:
                if t == 0:
                    act(G("ag0", gi, 16), IND(own(0, *GR[gi]), su))
                act(G("jv%d" % t, gi, 16), IND(A("jc"), su))
        if t < 2:
            cp(A("kf%d" % t), A("e%d" % t))
        if pas == 1 and t == 0:
            act(A("cf0"), A("c0"))
            act(A("cq0"), A("c0"), AF.Identity, bias=1536.0)

    def lists2(pas, kout):
        tt(A("w0"), A("j0"), A("j1"), OP.mult)
        tt(A("w1"), A("j0"), A("j1"), OP.add)
        ts(A("w0"), A("w0"), 0.0, OP.is_equal)
        ts(A("w2"), A("w1"), 1.0, OP.is_equal)
        ts(A("w1"), A("w1"), -1.0, OP.mult, 6.0, OP.add)
        tt(A("w0"), A("w0"), A("w2"), OP.add)
        tt(A("w1"), A("w1"), A("base"), OP.add)
        tt(A("lo"), A("w0"), A("base"), OP.add)
        tt(A("hi"), A("w1"), A("w0"), OP.subtract)
        cp(A("lou"), A("lo"))
        cp(A("hiu"), A("hi"))
        for gi in GI:
            for src, dst, co in (("lou", "glo", "cl"), ("hiu", "ghi", "ch")):
                ts(G(dst, gi, 16), IND(G("tri32", gi, 64), G(src, gi, 1)), -1536.0, OP.add)
                if pas == 1:
                    act(G(co, gi, 16), IND(G("ck", gi, 64), G(src, gi, 1)))
        for gi in GI:
            for s, dst in enumerate(("lx", "ly")):
                b = "ps%d" % (2 + s + 4 * gi)
                for u0, u1 in R2:
                    n = 8 * (u1 - u0)
                    for x, src in enumerate(("glo", "ghi") if group(u0) == gi else ()):
                        for e in range(2):
                            mm(A(b, 16 * u0 + n * x, 16 * u0 + n * x + n), A("p%d%d" % (s, e)),
                               A(src, 16 * u0 + e, 16 * u1, 2), e == 0, e == 1)
                ts(G(dst, gi, 16), A(b, 16 * GR[gi][0], 16 * GR[gi][1]), 1536.0, OP.add)
        for gi in GI:
            w = 64 * (GR[gi][1] - GR[gi][0])
            b = A("ps%d" % gi, 0, w)
            mm(b, ONE1, A("km", 0, w, p1=1), True, False)
            mm(b, A("gm1"), G("fl1", gi, 64), False, False)
            mm(b, ONE1, A("kn", 0, w, p1=1), False, False)
            mm(b, A("gm"), G("fl0", gi, 64), False, False)
            mm(b, A("ib"), G("phib", gi, 64), False, True)
            act(own(kout, *GR[gi]), b)

    def round2(pas, kin, kout):
        tab = A("tab%d" % kin)
        now.update(step=kin, side=None)
        for u0, u1 in R2:
            gi = group(u0)
            cuts = [x for x in C2 if 16 * u0 <= x <= 16 * u1]
            solo = SOLO if u1 == 12 else 0
            x1 = 8 * (u0 + u1)
            x0 = x1 - solo
            if solo:
                pair_gathers(tab, kin, "lx", "ly", [x for x in cuts if x < x0] + [x0])
                cuts = [x for x in cuts if x >= x1]
                pair_gathers(tab, kin, "lx", "ly", cuts[:AHEAD + 1])
                cuts = cuts[AHEAD:]
                act(A("ga", 16 * x0, 16 * x1), IND(tab, A("lx", x0, x1)), ext=kin)
                act(A("zb", 0, 16 * solo), IND(tab, A("ly", x0, x1)), ext=kin)
                mm(A("ps4", 0, 16 * solo), A("ib"), A("ga", 16 * x0, 16 * x1), True, False)
                mm(A("ps4", 0, 16 * solo), A("nib"), A("zb", 0, 16 * solo), False, True)
                act(A("db", 0, 16 * solo), A("ps4", 0, 16 * solo), AF.Relu)
            pair_gathers(tab, kin, "lx", "ly", cuts)
            n, c = 16 * (u1 - u0), 16 * (u0 - GR[gi][0])
            o = A("ps%d" % (5 + gi), c, c + n)
            mm(o, B16, A("bd", 0, n, p1=16), True, False)
            if pas == 1:
                mm(o, A("i1k"), U("cl", u0, u1, 16), False, False)
                mm(o, A("ni1k"), U("ch", u0, u1, 16), False, False)
            for r in range(16):
                x = 256 * u0 + 8 * n * (r // 8)
                if r < 8 and solo:
                    part = A(o[0], o[2] - 2 * solo, o[2])
                    if 2 * solo < n:
                        mm(A(o[0], o[1], part[1]), A("gp"), A("mn", x + r, 16 * x0, 8), False, False)
                    mm(part, A("gp"), A("ga", 16 * x0 + r, 16 * x1, 8), False, False)
                    mm(part, A("gn"), A("db", r, 16 * solo, 8), False, False)
                else:
                    mm(o, A("gp" if r < 8 else "gn"), A("mn", x + r % 8, x + 8 * n, 8), False, r == 15)
            for gi in ends(u1):
                n = 16 * (GR[gi][1] - GR[gi][0])
                scan(G("sc2", gi, 16), A("r16s", 0, n), A("ps%d" % (5 + gi), 0, n), OP.max)
                tt(G("y2", gi, 1), A("sc2", 16 * GR[gi][0] + 15, 16 * GR[gi][1], 16), G("lo", gi, 1), OP.max)
                tt(G("si2", gi, 1), G("y2", gi, 1), G("hi", gi, 1), OP.min)
                cp(G("su2", gi, 1), G("si2", gi, 1))
                cp(IND(own(kout, *GR[gi]), G("su2", gi, 1)), A("mark", 0, n))
                send_done(kout, u1, S2)
        now.update(side=kout)

    def marks(t, tab, ext):
        for u in range(0, 12, 2):
            if t == 0 and u == LATE:
                now.update(side=now["side"] + 1)
            o = A("mn", NW * t + 256 * u, NW * t + 256 * u + 512)
            (act if TG[t][u // 2] == "a" else cp)(o, IND(tab, U("e%d" % t, u, u + 2, 16)), ext=ext)
            if TG[t][u // 2] in TG[t][:u // 2]:
                ops[-1]["behind"] = len(ops) - 1 - u // 2 + TG[t].rindex(TG[t][u // 2], 0, u // 2)

    def places(t):
        for i, (u0, u1, _) in enumerate(LP):
            b = A("ps%d" % (4 + i), 0, 16 * (u1 - u0))
            mm(b, A("ih"), U("qh%d" % t, u0, u1, 16), True, False)
            for r in range(16):
                mm(b, A("dm", 128 * r, 128 * r + 128), A("mn", NW * t + 256 * u0 + r, NW * t + 256 * u1, 16), False, r == 15)
            if i < 2:
                place(t, i)

    def place(t, i):
        u0, u1, _ = LP[i]
        tt(U("tq", u0, u1, 16), A("ps%d" % (4 + i), 0, 16 * (u1 - u0)), U("kf%d" % t, u0, u1, 16), OP.max)
        ts(U("f%d" % t, u0, u1, 16), U("tq", u0, u1, 16), float(NONE if t else NEW[1] + NV - 1), OP.min)

    def level(pas, t, kin, kout):
        tab = A("tab%d" % (6 * pas + 3), 0, (NEW[1] + NV, NEW[1], NW)[t])
        need_p = not (pas == 0 and t == 0)
        lst, c = "e2" if t == 2 else "f%d" % t, "c%d" % t
        ext = kin
        now.update(step=kin, side=kin)
        for u0, u1, halves in LP:
            n = 16 * (u1 - u0)
            for b, m0, m1 in halves:
                mm(A("ps%d" % b, 0, n * (m1 - m0)), ONE1, A("ke", 0, n * (m1 - m0), p1=1), True, False)
                for m in range(m1 - m0):
                    mm(A("ps%d" % b, n * m, n * m + n), A("nib"), U(c, u0, u1, 16), False, False)
        now.update(side=None)

        def opening(gi, h):
            n = 16 * (GR[gi][1] - GR[gi][0])
            if need_p:
                mm(A("ps%d" % (3 + gi), 0, n), ONE33, A("kl", 0, n, p1=33), True, False)
                mm(A("ps%d" % (3 + gi), 0, n), A("ib"), G(c, gi, 16), False, False)
            mm(A("ps%d" % (5 + gi), 0, n), ONE1, A("kx", 0, n, p1=1), True, False)

        def part(name, i, m0, m1):
            u0, u1, _ = LP[i]
            return A(name, 128 * u0 + 16 * (u1 - u0) * m0, 128 * u0 + 16 * (u1 - u0) * m1)

        def ebank(i, h):
            b, m0, m1 = LP[i][2][h]
            return A("ps%d" % b, 0, 16 * (LP[i][1] - LP[i][0]) * (m1 - m0))

        def fetch(i, h):
            u0, u1, halves = LP[i]
            n, x = 16 * (u1 - u0), 16 * u0
            if t < 2 and i == 1:
                last = max(j for j in range(len(ops)) if ops[j]["q"] == "v")
                place(t, 2)
                ops[-2]["behind"] = last
            for e, cols in LG[i]:
                (act if e == "a" else cp)(A("ga", 16 * x, 16 * (x + cols)), IND(tab, A(lst, x, x + cols)), ext=ext)
                x += cols
            for b, m0, m1 in halves:
                for r in range(2 * m0, 2 * m1):
                    x = n * (r // 2 - m0)
                    mm(A("ps%d" % b, x, x + n), A("ib"), A("ga", 256 * u0 + r, 256 * u1, 16), False, r == 2 * m1 - 1)

        def z(i, h):
            if (i, h) in ZV:
                ts(part("zb", i, *LP[i][2][h][1:]), ebank(i, h), 0.5, OP.add)
            else:
                act(part("zb", i, *LP[i][2][h][1:]), ebank(i, h), AF.Identity, bias=0.5)

        def dif(i, h):
            ms_ = LP[i][2][h][1:]
            tt(part("db", i, *ms_), ebank(i, h), part("zb", i, *ms_), OP.subtract)

        def size(i, h):
            ms_ = LP[i][2][h][1:]
            if (i, h) not in RELU:
                act(part("ab", i, *ms_), part("db", i, *ms_), AF.Abs)
            else:
                ts(part("ab", i, *ms_), part("db", i, *ms_), 0.0, OP.max)

        def bound(i, h):
            ms_ = LP[i][2][h][1:]
            if group(LP[i][0]) not in THC:
                ts(part("tb", i, *ms_), part("zb", i, *ms_), float(2 ** 20), OP.is_lt, A("thf", 2, 3), OP.mult)

        def limit(gi, h):
            if gi not in THC:
                return
            b = A("ps%d" % gi, 0, 64)
            rows = [(i, m) for i in range(len(LP)) if group(LP[i][0]) == gi for m in range(8)]
            for r, (i, m) in enumerate(rows):
                mm(b, A("dm", 128 * r, 128 * r + 128), part("zb", i, m, m + 1), r == 0, r == len(rows) - 1)
            ts(A("vf", 64 * gi, 64 * gi + 64), b, 2.0 ** -30, OP.is_lt)

        def sums(i, h, turn=False):
            u0, u1, halves = LP[i]
            gi = group(u0)
            n, o = 16 * (u1 - u0), 16 * (u0 - GR[gi][0])
            _, m0, m1 = halves[h]
            tb, xb = A("ps%d" % (3 + gi), o, o + n), A("ps%d" % (5 + gi), o, o + n)
            terms = (("xn", "db"), ("xp2", "ab")) if (i, h) in RELU else (("xp", "ab"),)
            if turn:
                if need_p:
                    for m in range(m0, m1):
                        mm(tb, A("lu"), part("db", i, m, m + 1), False, m == 7 and bool(ends(u1)))
                    if m1 == 8:
                        for gi in ends(u1):
                            phases(t, gi)
                return
            last = m1 == 8 and bool(ends(u1))
            if gi not in THC:
                terms = (("xn", "tb"),) + terms
            if last and gi in THC:
                for x in range(0, o + 1, 64):
                    for l in ("th", "tl"):
                        mm(A(xb[0], x, x + 64), A(l + str(x // 64)), A("vf", 64 * gi, 64 * gi + 64), False, False)
            for j, (l, r) in enumerate(terms):
                for m in range(m0, m1):
                    mm(xb, A(l), part(r, i, m, m + 1), False, last and j == len(terms) - 1 and m == 7)
            if m1 == 8:
                for gi in ends(u1):
                    finish(pas, t, kout, gi)

        call = {"f": fetch, "z": z, "d": dif, "a": size, "l": limit, "s": sums, "b": bound, "o": opening,
                "t": lambda i, h: sums(i, h, True)}
        for w in LO.split():
            if t < 2:
                for f in later.pop(w, []):
                    n = len(ops)
                    f()
                    ops[n]["behind"] = max(j for j in range(n) if ops[j]["q"] == ops[n]["q"] and ops[j]["side"] is None)
            call[w[0]](int(w[1]), int(w[2:] or 0))

    def phases(t, gi):
        tb = A("ps%d" % (3 + gi), 0, 16 * (GR[gi][1] - GR[gi][0]))
        if gi in ZZV:
            ts(G("zz", gi, 16), tb, -1663.5, OP.add)
        else:
            act(G("zz", gi, 16), tb, AF.Identity, bias=-1663.5)
        tt(G("rr%d" % t, gi, 16), tb, G("zz", gi, 16), OP.subtract)

    def finish(pas, t, kout, gi):
        n = 16 * (GR[gi][1] - GR[gi][0])
        tb, xb = A("ps%d" % (3 + gi), 0, n), A("ps%d" % (5 + gi), 0, n)
        su = G("su%d" % t, gi, 1)

        def h(name):
            return G(name + (str(t) if name in ("rr", "mk", "nk") else ""), gi, 16)
        if t > 0:
            o = NEW[t] + 192 * rank
            new = A("tab%d" % (6 * pas + 3), o + 16 * GR[gi][0], o + 16 * GR[gi][1])
            ts(h("pb"), xb, MARK, OP.min, -1536.0, OP.max)
            tt(new, h("rr"), h("pb"), OP.add)
            if GR[gi][1] == 12:
                send(kout, A(new[0], o, o + 192))
            now.update(side=kout)
        if t == 0:
            ts(h("nk"), xb, 0.0, OP.is_le)
        elif pas == 1:
            ts(h("nk"), xb, 0.0, OP.is_le, 512.0, OP.mult)
        if pas == 0:
            if t == 0:
                tt(IND(own(6, *GR[gi]), su), h("ag0"), h("nk"), OP.mult)
                send_done(kout, GR[gi][1], SL)
                now.update(side=kout)
            ts(h("mk"), xb, 0.0, OP.is_gt, MARK, OP.mult)
            if t == 2 and gi in CKG:
                later[GAP].append(lambda: tt(IND(G("ck", gi, 64), su), h("jv2"), h("mk"), OP.mult))
            elif t == 2:
                now.update(side=kout + CKW)
                tt(IND(G("ck", gi, 64), su), h("jv2"), h("mk"), OP.mult)
            else:
                tt(IND(G("ck", gi, 64), su), h("jv%d" % t), h("mk"), OP.mult)
        elif t == 0:
            tt(h("dd"), h("rr"), h("cq0"), OP.subtract)
            tt(h("tt"), h("dd"), h("nk"), OP.mult)
            tt(IND(G("pout", gi, 64), su), h("tt"), h("cf0"), OP.add)
            store(T.yphi[:, 64 * GR[gi][0]:64 * GR[gi][1]], G("pout", gi, 64), "d_y%d" % gi)
        now.update(side=None)

    def record(t):
        b = A("ps%d" % (2 if t == 2 or R1 else 3), 0, 192)
        mm(b, A("ib"), A("c%d" % t), True, False)
        mm(b, A("ib"), A("nk%d" % t), False, True)
        tt(A("tq%d" % t), b, A("tab9", NEW[t] + 192 * rank, NEW[t] + 192 * rank + 192), OP.min)
        for gi in GI[:3 - t]:
            put(t, gi)

    def put(t, gi):
        cp(IND(G("pout", gi, 64), G("su%d" % t, gi, 1)), G("tq%d" % t, gi, 16))
        ops[-1]["cap"] = len(ops)

    for pas in range(2):
        k = 6 * pas
        round01(pas, 0, k, k + 1)
        prep_level(pas, 0)
        round01(pas, 1, k + 1, k + 2)
        lists2(pas, k + 3)
        prep_level(pas, 1)
        round2(pas, k + 2, k + 3)
        prep_level(pas, 2)
        if pas == 1:
            for gi in GI:
                w = 64 * (GR[gi][1] - GR[gi][0])
                b = A("ps%d" % (5 + gi), 0, w)
                mm(b, ONE1, A("kv", 0, w, p1=1), True, False)
                mm(b, A("g3"), G("fl0", gi, 64), False, False)
                mm(b, A("g2"), G("fl1", gi, 64), False, False)
                mm(b, A("i70"), own(k + 3, *GR[gi]), False, True)
                act(G("lev", gi, 64), b, AF.Relu)
            rec("s", lambda: g.sync.dma_start(T.ylev[:], T.lev[0:128:16, :]), [], [A("lev")], 0.1, sem="d_lev", lag=LAT)
        later[GAP] = [lambda: record(2)] if pas else []
        level(pas, 2, k + 3, k + 4)
        now.update(side=k + 4)
        marks(1, A("tab%d" % (k + 3), 0, NW), k + 3)
        places(1)
        marks(0, A("tab%d" % (k + 3), 0, NW), k + 3)
        level(pas, 1, k + 4, k + 5)
        now.update(side=k + 5)
        places(0)
        if pas == 0:
            later[GAP], later["o0"] = [], []
            for gi in GI:
                b = A("ps%d" % (3 + gi), 0, 64 * (GR[gi][1] - GR[gi][0]))
                later["o0"].append(lambda gi=gi, b=b: (mm(b, A("ib"), own(0, *GR[gi]), True, False),
                                                       mm(b, A("ib"), G("ck", gi, 64), False, True)))
                later[GAP].append(lambda gi=gi, b=b: ts(own(6, *GR[gi]), b, 0.0, OP.max))
        elif R1:
            later[GAP] = [lambda: record(1)]
        else:
            last = max(j for j in range(len(ops)) if ops[j]["q"] == "v")
            record(1)
            ops[-3]["behind"] = last
            later[GAP] = [lambda: put(2, 1)]
        level(pas, 0, k + 5, k + 6)

    emit(g, T, ops, sends, per_send)


def emit(g, T, ops, sends, per_send):
    hist, bank = {}, {}
    for i, o in enumerate(ops):
        deps, after = set(), {}
        touched = [(d, False) for d in o["rd"]] + [(d, True) for d in o["wr"]]
        for d, w in touched:
            if d[0].startswith("ps"):
                j = bank.get(d[0])
                if j is not None and j != i:
                    if ops[j]["q"] == o["q"]:
                        after[j] = 0.0
                    else:
                        deps.add(j)
                bank[d[0]] = i
            else:
                for (lo, hi, j, jw) in hist.setdefault(d[0], []):
                    if (w or jw) and lo < d[2] and d[1] < hi and j != i:
                        deps.add(j)
        for d, w in touched:
            if not d[0].startswith("ps"):
                h = hist[d[0]]
                if w and d[3] == 1 and d[4] == 0 and d[5] == 128:
                    h[:] = [e for e in h if not (d[1] <= e[0] and e[1] <= d[2])]
                h.append((d[1], d[2], i, w))
        for j in deps:
            after[j] = HOP if ops[j]["sem"] == "none" else ops[j]["lag"]
        for k in o["ext"]:
            js = sends[k]
            for n, j in enumerate(js):
                after[j] = WAY + sum(ops[x]["lag"] for x in js[n:])
        if "behind" in o:
            after.setdefault(o["behind"], 0.0)
        o["deps"], o["after"], o["succ"] = deps, after, []
    allsends = sorted(j for js in sends.values() for j in js)
    for a, b in zip(allsends[:-1], allsends[1:]):
        ops[b]["after"].setdefault(a, 0.0)
    for i, o in enumerate(ops):
        for j in o["after"]:
            ops[j]["succ"].append(i)
    for o in reversed(ops):
        o["due"] = o["step"] if o["side"] is None else min([99] + [ops[s]["due"] for s in o["succ"]])
    for i in range(len(ops) - 1, -1, -1):
        o = ops[i]
        o["rank"] = i if o["side"] is None else min([o.get("cap", len(ops))] + [ops[s]["rank"] for s in o["succ"]])
    closing = {js[-1]: k for k, js in sends.items() if k < 12}
    owed, todo = {}, {}
    opening = {}
    for i, o in enumerate(ops):
        if o["side"] is None:
            opening.setdefault(o["step"], i)
    for o in ops:
        if o["side"] is not None:
            o["urgent"] = o["rank"] < len(ops) and bool(ops[o["rank"]]["ext"])
            owed[o["q"], o["due"]] = owed.get((o["q"], o["due"]), 0) + o["urgent"]
        else:
            todo[o["q"], o["step"]] = todo.get((o["q"], o["step"]), 0) + 1
    sent, end = -1, LAT - 0.3
    free = {q: 0.0 for q in "vapgs"}
    done = {q: 0.0 for q in "vapgs"}
    left = [len(o["after"]) for o in ops]
    ready = {i: 0.0 for i, n in enumerate(left) if n == 0}
    order = []
    while ready:
        best = None
        for q in free:
            main = [j for j in ready if ops[j]["q"] == q and ops[j]["side"] is None]
            t = max(free[q], min([ready[j] for j in main], default=1e9))
            pick = min([j for j in main if ready[j] <= t + HOP], default=None)
            at = 1e9 if pick is None else max(free[q], ready[pick])
            pause, limit = sent, end
            if sent >= 0 and not todo.get((q, sent)):
                pause, limit = sent + 1, done[q] + EARLY + ROOM
            fill = []
            for j in ready:
                o = ops[j]
                if o["q"] == q and o["side"] is not None and min(o["side"], o["due"]) <= pause:
                    s = max(free[q], ready[j])
                    fits = s + o["cost"] <= min(at, limit + (q in "gp")) + HOP
                    if o["due"] <= pause:
                        ok = s <= at and (s + o["cost"] <= at + HOP or pick is None or o["rank"] < pick)
                    else:
                        ok = fits and (pause < 1 or not owed.get((q, pause)))
                    if ok or pause == 12:
                        fill.append((round(s, 1), o["rank"], j))
            if fill and min(fill)[0] <= at:
                at, _, pick = min(fill)
            if pick is not None and (best is None or at < best[0]):
                best = (at, pick)
        i = best[1]
        q = ops[i]["q"]
        start = max(ready.pop(i), free[q])
        ops[i]["end"] = free[q] = start + ops[i]["cost"]
        if ops[i]["side"] is not None:
            owed[q, ops[i]["due"]] -= ops[i]["urgent"]
        else:
            todo[q, ops[i]["step"]] -= 1
            done[q] = free[q]
        if i in closing:
            sent, end = closing[i], start + ROOM * (1 if closing[i] else ROOM0)
        order.append(i)
        for s in ops[i]["succ"]:
            left[s] -= 1
            if left[s] == 0:
                ready[s] = max(ops[j]["end"] + lag for j, lag in ops[s]["after"].items())
    seq, place = {}, {}
    known = {q: {} for q in "vapgs"}
    for n, i in enumerate(order):
        o = ops[i]
        place[i] = n
        kn = known[o["q"]]
        waits = []
        for k in o["ext"]:
            s, v = "arr%d" % k, per_send * len(sends[k])
            if kn.get(s, 0) < v:
                waits.append((s, v))
                kn[s] = v
        for j in sorted(o["deps"], key=lambda j: -place[j]):
            if ops[j]["sem"] == "none":
                raise ValueError("a table that is being sent is written again")
            key, val = ops[j]["done"]
            if kn.get(key, 0) >= val:
                continue
            waits.append(j)
            ops[j]["need"] = True
            for k2, v2 in ops[j]["clock"].items():
                if kn.get(k2, 0) < v2:
                    kn[k2] = v2
            kn[key] = val
        o["waits"] = waits
        o["clock"] = dict(kn)
        key = o["sem"] or o["q"]
        seq[key] = seq.get(key, 0) + (16 if o["sem"] else 1)
        o["done"] = (key, seq[key])
    eng = {"v": g.vector, "a": g.scalar, "p": g.tensor, "g": g, "s": g.sync}
    cnt = {}
    for i in order:
        o = ops[i]
        q = o["q"]
        for w in o["waits"]:
            s, v = w if isinstance(w, tuple) else ops[w]["sig"]
            eng[q].wait_ge(T.sem[s], v)
        ins = o["fn"]()
        if o["sem"] == "none":
            continue
        if o["sem"]:
            ins.then_inc(T.sem[o["sem"]], 16)
            o["sig"] = o["done"]
        elif o.get("need"):
            cnt[QSEM[q]] = cnt.get(QSEM[q], 0) + 1
            ins.then_inc(T.sem[QSEM[q]], 1)
            o["sig"] = (QSEM[q], cnt[QSEM[q]])
    g.wait_ge(T.sem.sent, per_send * len(allsends))
    for s in ("d_lev", "d_y0", "d_y1"):
        g.sync.wait_ge(T.sem[s], 16)
